import numpy as np
import ml_dtypes


def mxq(x, axis, fmt="e4m3"):
    dtype, down = {"e4m3": (ml_dtypes.float8_e4m3fn, 7), "e5m2": (ml_dtypes.float8_e5m2, 14)}[fmt]
    v = np.moveaxis(np.asarray(x, np.float32).astype(ml_dtypes.bfloat16).astype(np.float64), axis, -1)
    blocks = v.reshape(v.shape[:-1] + (-1, 32))
    amax = np.abs(blocks).max(-1, keepdims=True)
    byte = np.maximum(np.where(amax > 0, np.frexp(amax)[1] - 1 + 127, 0) - down, 1)
    scale = np.exp2(byte - 127.0)
    codes = (blocks / scale).astype(np.float32).astype(dtype).astype(np.float64)
    return np.moveaxis((codes * scale).reshape(v.shape), -1, axis)


WIDE = False


def mx_kscale(k):
    if not WIDE:
        return np.ones(k)
    levels = np.array([10, -10, 5, -5, 0])
    if k % 512:
        return np.exp2(np.random.permutation(np.resize(levels, k // 32))).repeat(32)
    a = np.empty((k // 512, 16))
    for p in range(k // 512):
        a[p, :8] = np.random.permutation(np.resize(levels, 8))
        for g in range(8):
            far = levels[np.abs(levels - a[p, g]) >= 10]
            a[p, g + 8] = far[np.random.randint(len(far))]
    return np.exp2(a.ravel()).repeat(32)


def f64(x):
    return np.asarray(x).astype(np.float64)


def striped(idx):
    return np.tile(idx.reshape(-1, 16).T, (8, 1)).astype(np.uint16)


def unstriped(offs):
    return offs[:16].T.reshape(-1).astype(np.int64)


def pack_weight(w):
    k, n = w.shape
    w = f64(np.asarray(w, np.float32).astype(ml_dtypes.bfloat16)).reshape(k // 32, 32, n)
    amax = np.abs(w).max(1)
    byte = np.clip(np.where(amax > 0, np.frexp(amax)[1] - 1 + 127 - 7, 1), 1, 254)
    scaled = (w * np.exp2(127.0 - byte)[:, None, :]).reshape(k, n).astype(np.float32)
    words = np.ascontiguousarray(scaled.reshape(k // 512, 128, 4, n).transpose(0, 1, 3, 2)).astype(ml_dtypes.float8_e4m3fn).view(np.uint8)
    return words, np.ascontiguousarray(byte.astype(np.uint8).reshape(k // 512, 16, n))


def unpack_weight(words, scales):
    g, p, n, _ = words.shape
    vals = np.ascontiguousarray(words).view(ml_dtypes.float8_e4m3fn).astype(np.float64) * np.repeat(np.exp2(scales.astype(np.float64) - 127.0), 8, axis=1)[..., None]
    return vals.transpose(0, 1, 3, 2).reshape(g * 512, n)


def planes(y):
    n, m = y.shape
    v = y.astype(np.float32).astype(ml_dtypes.bfloat16).astype(np.float64).reshape(n // 32, 32, m)
    top = np.abs(v).max(1)
    byte = np.clip(np.where(top > 0, np.frexp(top)[1] - 1 + 127 - 7, 1), 1, 254)
    codes = (v * np.exp2(127.0 - byte)[:, None, :]).reshape(n, m).astype(np.float32).astype(ml_dtypes.float8_e4m3fn).view(np.uint8)
    words = codes.reshape(n // 512, 128, 4, m).transpose(0, 1, 3, 2)
    return np.ascontiguousarray(words), np.ascontiguousarray(byte.astype(np.uint8).reshape(n // 512, 16, m))


def silu(v):
    return v / (1.0 + np.exp(-np.maximum(v, -700.0)))


K, T, S, N = 512, 2048, 512, 512


def setup_inputs():
    n = np.random.standard_normal
    s = mx_kscale(K)[:, None]
    packed_xT = pack_weight(n((K, T)) * s)
    return {
        "x_words": packed_xT[0],
        "x_scales": packed_xT[1],
        "w1": (n((K, N)) / np.sqrt(K) / s).astype(np.float32),
        "w2": (n((K, N)) / np.sqrt(K) / s).astype(np.float32),
        "feat": (n((N, S))).astype(np.float32),
        "offs": striped(np.random.permutation(T)[:S]),
    }


def reference(x_words, x_scales, w1, w2, feat, offs):
    xq = unpack_weight(x_words, x_scales)[:, unstriped(offs)]
    g = mxq(f64(w1), 0, "e4m3").T @ xq
    h = mxq(f64(w2), 0, "e4m3").T @ xq
    out_0 = silu(f64(feat) + f64(feat) * g + h)
    return (out_0,) + planes(out_0)

@@ -1,0 +1,159 @@
+from contextlib import ExitStack
+
+import concourse.mybir as mybir
+
+K, T, S, N = 512, 2048, 512, 512
+FLOPS = 2 * 2 * K * N * S
+
+F32 = mybir.dt.float32
+BF16 = mybir.dt.bfloat16
+I32 = mybir.dt.int32
+U32 = mybir.dt.uint32
+U16 = mybir.dt.uint16
+U8 = mybir.dt.uint8
+FP8X4 = mybir.dt.float8_e4m3fn_x4
+ADD = mybir.AluOpType.add
+MULT = mybir.AluOpType.mult
+SILU = mybir.ActivationFunctionType.Silu
+
+P = 128
+PACK = 4
+HALF = S // 2
+CH = 128
+NCH = S // CH
+
+
+def tile_picked_zfilm_silu_po_kernel(tc, x_words, x_scales, w1, w2, feat, offs, out_0, out_1, out_2):
+    nc = tc.nc
+    with ExitStack() as ctx:
+        keep = ctx.enter_context(tc.tile_pool(name="keep", bufs=1))
+        psum = ctx.enter_context(tc.psum_pool(name="psum", bufs=1))
+
+        offsets = keep.tile([P, S // 16], U16, name="offsets")
+        nc.sync.dma_start(offsets[:], offs)
+
+        table_scales = keep.tile([P, T], U8, name="table_scales", align_bytes=64)
+        nc.vector.memset(table_scales[:].bitcast(I32), 0)
+        for q in range(4):
+            nc.scalar.dma_start(table_scales[32 * q : 32 * q + 4, :].bitcast(I32), x_scales[0, 4 * q : 4 * q + 4, :].bitcast(I32))
+
+        w_raw = []
+        for i, w in enumerate((w1, w2)):
+            raw = keep.tile([P, PACK, N], F32, name="w_raw%d" % i)
+            nc.sync.dma_start(raw[:], w.rearrange("(p j) c -> p j c", j=PACK))
+            w_raw.append(raw)
+        table_words = keep.tile([P, T], U32, name="table_words", align_bytes=64)
+        nc.sync.dma_start(table_words[:].bitcast(I32), x_words[0].rearrange("p n t -> p (n t)").bitcast(I32))
+        feat_rows = feat.rearrange("(p t) s -> p t s", t=PACK)
+        feat_sb = []
+        for h in range(2):
+            f = keep.tile([P, PACK, HALF], F32, name="feat%d" % h)
+            nc.sync.dma_start(f[:], feat_rows[:, :, h * HALF : (h + 1) * HALF])
+            feat_sb.append(f)
+
+        x_sc = keep.tile([P, S], U8, name="x_sc", align_bytes=64)
+        nc.vector.tensor_copy(x_sc[:], table_scales[:].indirect(offsets[:]))
+
+        w_codes = []
+        w_scales = []
+        for i in range(2):
+            dealt = w_raw[i][:].rearrange("p j (m t) -> p m t j", t=PACK)
+            rounded = []
+            for u in range(2):
+                wb = keep.tile([P, 2 * P * PACK], BF16, name="wb%d%d" % (i, u), align_bytes=64)
+                dst = wb[:].rearrange("p (t m j) -> p m t j", t=2, j=PACK)
+                if u == 0:
+                    nc.vector.tensor_copy(dst, dealt[:, :, 0:2, :])
+                else:
+                    nc.scalar.copy(dst, dealt[:, :, 2:4, :])
+                rounded.append(wb)
+            for u in range(2):
+                codes = keep.tile([P, 2 * P], U32, name="wc%d%d" % (i, u), align_bytes=64)
+                scales = keep.tile([P, 2 * P], U8, name="ws%d%d" % (i, u), align_bytes=64)
+                nc.vector.quantize_mx(out=codes[:].bitcast(FP8X4), scales=scales[:], in_=rounded[u][:])
+                w_codes.append(codes)
+                w_scales.append(scales)
+
+        x_codes = []
+        for h in range(2):
+            xc = keep.tile([P, HALF], U32, name="x_codes%d" % h, align_bytes=64)
+            nc.vector.tensor_copy(xc[:], table_words[:].indirect(offsets[:, h * (HALF // 16) : (h + 1) * (HALF // 16)]))
+            x_codes.append(xc)
+
+        def product(i, c):
+            bank = psum.tile([P, PACK, CH], F32, name="bank%d%d" % (i, c))
+            h, o = divmod(c * CH, HALF)
+            for t in range(PACK):
+                u, e = divmod(t, 2)
+                nc.tensor.matmul_mx(
+                    out=bank[:, t, :],
+                    lhsT=w_codes[2 * i + u][:, e * P : (e + 1) * P].bitcast(FP8X4),
+                    lhsT_scale=w_scales[2 * i + u][:, e * P : (e + 1) * P],
+                    rhs=x_codes[h][:, o : o + CH].bitcast(FP8X4),
+                    rhs_scale=x_sc[:, c * CH : (c + 1) * CH],
+                    start=True,
+                    stop=True,
+                )
+            return bank
+
+        y_codes = keep.tile([P, S], U32, name="y_codes", align_bytes=64)
+        y_scales = keep.tile([P, S], U8, name="y_scales", align_bytes=64)
+        out_rows = out_0.rearrange("(p t) s -> p t s", t=PACK)
+        out_words = out_1[0].rearrange("p n t -> p (n t)")
+
+        v = {}
+        u_sb = {}
+        y = {}
+        yb = {}
+
+        def modulate(c):
+            g = product(0, c)
+            h, o = divmod(c * CH, HALF)
+            v[c] = keep.tile([P, PACK, CH], F32, name="v%d" % c)
+            nc.vector.scalar_tensor_tensor(v[c][:], g[:], 1.0, feat_sb[h][:, :, o : o + CH], ADD, MULT)
+
+        def shift(c):
+            hb = product(1, c)
+            u_sb[c] = keep.tile([P, PACK, CH], F32, name="u%d" % c)
+            nc.vector.tensor_tensor(u_sb[c][:], hb[:], v[c][:], ADD)
+            y[c] = keep.tile([P, PACK, CH], F32, name="y%d" % c)
+            nc.scalar.activation(y[c][:], u_sb[c][:], SILU)
+            nc.sync.dma_start(out_rows[:, :, c * CH : (c + 1) * CH], y[c][:])
+
+        def round_y(c, on_vector):
+            yb[c] = keep.tile([P, CH * PACK], BF16, name="yb%d" % c, align_bytes=64)
+            dst = yb[c][:].rearrange("p (a i t) -> p a t i", i=4, t=PACK)
+            src = y[c][:].rearrange("p t (a i) -> p a t i", i=4)
+            if on_vector:
+                nc.vector.tensor_copy(dst, src)
+            else:
+                nc.scalar.copy(dst, src)
+
+        def quantise_y(c):
+            cols = slice(c * CH, (c + 1) * CH)
+            nc.vector.quantize_mx(out=y_codes[:, cols].bitcast(FP8X4), scales=y_scales[:, cols], in_=yb[c][:])
+
+        def store_words(a, b):
+            nc.sync.dma_start(out_words[:, PACK * a : PACK * b].bitcast(I32), y_codes[:, a:b].bitcast(I32))
+
+        modulate(0)
+        modulate(1)
+        shift(0)
+        round_y(0, False)
+        shift(1)
+        round_y(1, False)
+        modulate(2)
+        modulate(3)
+        quantise_y(0)
+        shift(2)
+        shift(3)
+        quantise_y(1)
+        store_words(0, HALF)
+        round_y(2, True)
+        quantise_y(2)
+        round_y(3, True)
+        quantise_y(3)
+        store_words(HALF, S)
+        for q in range(4):
+            eng = nc.scalar if q % 2 == 0 else nc.sync
+            eng.dma_start(out_2[0, 4 * q : 4 * q + 4, :].bitcast(I32), y_scales[32 * q : 32 * q + 4, :].bitcast(I32))

@@ -14,6 +14,7 @@ U8 = mybir.dt.uint8
 FP8X4 = mybir.dt.float8_e4m3fn_x4
 ADD = mybir.AluOpType.add
 MULT = mybir.AluOpType.mult
+COPY = mybir.ActivationFunctionType.Copy
 SILU = mybir.ActivationFunctionType.Silu
 
 P = 128
@@ -31,19 +32,15 @@ def tile_picked_zfilm_silu_po_kernel(tc, x_words, x_scales, w1, w2, feat, offs, 
 
         offsets = keep.tile([P, S // 16], U16, name="offsets")
         nc.sync.dma_start(offsets[:], offs)
-
-        table_scales = keep.tile([P, T], U8, name="table_scales", align_bytes=64)
-        nc.vector.memset(table_scales[:].bitcast(I32), 0)
+        staged_scales = keep.tile([P, T], U8, name="staged_scales", align_bytes=64)
         for q in range(4):
-            nc.scalar.dma_start(table_scales[32 * q : 32 * q + 4, :].bitcast(I32), x_scales[0, 4 * q : 4 * q + 4, :].bitcast(I32))
-
-        w_raw = []
-        for i, w in enumerate((w1, w2)):
-            raw = keep.tile([P, PACK, N], F32, name="w_raw%d" % i)
-            nc.sync.dma_start(raw[:], w.rearrange("(p j) c -> p j c", j=PACK))
-            w_raw.append(raw)
+            nc.scalar.dma_start(staged_scales[32 * q : 32 * q + 4, :].bitcast(I32), x_scales[0, 4 * q : 4 * q + 4, :].bitcast(I32))
+        w1_raw = keep.tile([P, PACK, N], F32, name="w1_raw")
+        nc.sync.dma_start(w1_raw[:], w1.rearrange("(p j) c -> p j c", j=PACK))
         table_words = keep.tile([P, T], U32, name="table_words", align_bytes=64)
         nc.sync.dma_start(table_words[:].bitcast(I32), x_words[0].rearrange("p n t -> p (n t)").bitcast(I32))
+        w2_raw = keep.tile([P, PACK, N], F32, name="w2_raw", tag="w2_raw", align_bytes=64)
+        nc.sync.dma_start(w2_raw[:], w2.rearrange("(p j) c -> p j c", j=PACK))
         feat_rows = feat.rearrange("(p t) s -> p t s", t=PACK)
         feat_sb = []
         for h in range(2):
@@ -51,28 +48,38 @@ def tile_picked_zfilm_silu_po_kernel(tc, x_words, x_scales, w1, w2, feat, offs, 
             nc.sync.dma_start(f[:], feat_rows[:, :, h * HALF : (h + 1) * HALF])
             feat_sb.append(f)
 
+        table_scales = keep.tile([P, T], U8, name="table_scales", align_bytes=64)
+        nc.vector.memset(table_scales[:].bitcast(I32), 0)
+        for q in range(4):
+            nc.vector.tensor_copy(table_scales[32 * q : 32 * q + 4, :].bitcast(I32), staged_scales[32 * q : 32 * q + 4, :].bitcast(I32))
         x_sc = keep.tile([P, S], U8, name="x_sc", align_bytes=64)
         nc.vector.tensor_copy(x_sc[:], table_scales[:].indirect(offsets[:]))
 
-        w_codes = []
-        w_scales = []
+        rounded = {}
+        w_codes = {}
+        w_scales = {}
         for i in range(2):
-            dealt = w_raw[i][:].rearrange("p j (m t) -> p m t j", t=PACK)
-            rounded = []
             for u in range(2):
-                wb = keep.tile([P, 2 * P * PACK], BF16, name="wb%d%d" % (i, u), align_bytes=64)
-                dst = wb[:].rearrange("p (t m j) -> p m t j", t=2, j=PACK)
-                if u == 0:
-                    nc.vector.tensor_copy(dst, dealt[:, :, 0:2, :])
-                else:
-                    nc.scalar.copy(dst, dealt[:, :, 2:4, :])
-                rounded.append(wb)
+                rounded[i, u] = keep.tile([P, 2 * P * PACK], BF16, name="wb%d%d" % (i, u), tag="wb%d%d" % (i, u), align_bytes=64)
+
+        def round_w(i, raw, split):
+            dealt = raw[:].rearrange("p j (m t) -> p m t j", t=PACK)
+            dst = [rounded[i, u][:].rearrange("p (t m j) -> p m t j", t=2, j=PACK) for u in range(2)]
+            if split < P:
+                nc.vector.tensor_copy(dst[1][:, split:], dealt[:, split:, 2:4, :])
+            nc.scalar.copy(dst[1][:, :split], dealt[:, :split, 2:4, :])
+            nc.vector.tensor_copy(dst[0], dealt[:, :, 0:2, :])
+
+        def quantise_w(i):
             for u in range(2):
                 codes = keep.tile([P, 2 * P], U32, name="wc%d%d" % (i, u), align_bytes=64)
                 scales = keep.tile([P, 2 * P], U8, name="ws%d%d" % (i, u), align_bytes=64)
-                nc.vector.quantize_mx(out=codes[:].bitcast(FP8X4), scales=scales[:], in_=rounded[u][:])
-                w_codes.append(codes)
-                w_scales.append(scales)
+                nc.vector.quantize_mx(out=codes[:].bitcast(FP8X4), scales=scales[:], in_=rounded[i, u][:])
+                w_codes[2 * i + u] = codes
+                w_scales[2 * i + u] = scales
+
+        round_w(0, w1_raw, P)
+        quantise_w(0)
 
         x_codes = []
         for h in range(2):
@@ -96,32 +103,48 @@ def tile_picked_zfilm_silu_po_kernel(tc, x_words, x_scales, w1, w2, feat, offs, 
                 )
             return bank
 
-        y_codes = keep.tile([P, S], U32, name="y_codes", align_bytes=64)
+        g = {}
+        for c in (1, 0, 3, 2):
+            g[c] = product(0, c)
+        round_w(1, w2_raw, 84)
+        quantise_w(1)
+
         y_scales = keep.tile([P, S], U8, name="y_scales", align_bytes=64)
         out_rows = out_0.rearrange("(p t) s -> p t s", t=PACK)
         out_words = out_1[0].rearrange("p n t -> p (n t)")
 
         v = {}
+        g1 = {}
         u_sb = {}
         y = {}
         yb = {}
 
-        def modulate(c):
-            g = product(0, c)
+        def feat_of(c):
             h, o = divmod(c * CH, HALF)
-            v[c] = keep.tile([P, PACK, CH], F32, name="v%d" % c)
-            nc.vector.scalar_tensor_tensor(v[c][:], g[:], 1.0, feat_sb[h][:, :, o : o + CH], ADD, MULT)
+            return feat_sb[h][:, :, o : o + CH]
+
+        def modulate(c, tag):
+            v[c] = keep.tile([P, PACK, CH], F32, name="v%d" % c, tag=tag, align_bytes=64)
+            nc.vector.scalar_tensor_tensor(v[c][:], g[c][:], 1.0, feat_of(c), ADD, MULT)
+
+        def plus_one(c, tag):
+            g1[c] = keep.tile([P, PACK, CH], F32, name="g1%d" % c, tag=tag, align_bytes=64)
+            nc.scalar.activation(g1[c][:], g[c][:], COPY, bias=1.0)
+
+        def modulate_gpsimd(c, tag):
+            v[c] = keep.tile([P, PACK, CH], F32, name="v%d" % c, tag=tag, align_bytes=64)
+            nc.gpsimd.tensor_tensor(v[c][:], g1[c][:], feat_of(c), MULT)
 
         def shift(c):
             hb = product(1, c)
-            u_sb[c] = keep.tile([P, PACK, CH], F32, name="u%d" % c)
+            u_sb[c] = keep.tile([P, PACK, CH], F32, name="u%d" % c, tag="u%d" % c, align_bytes=64)
             nc.vector.tensor_tensor(u_sb[c][:], hb[:], v[c][:], ADD)
             y[c] = keep.tile([P, PACK, CH], F32, name="y%d" % c)
             nc.scalar.activation(y[c][:], u_sb[c][:], SILU)
             nc.sync.dma_start(out_rows[:, :, c * CH : (c + 1) * CH], y[c][:])
 
-        def round_y(c, on_vector):
-            yb[c] = keep.tile([P, CH * PACK], BF16, name="yb%d" % c, align_bytes=64)
+        def round_y(c, on_vector, tag):
+            yb[c] = keep.tile([P, CH * PACK], BF16, name="yb%d" % c, tag=tag, align_bytes=64)
             dst = yb[c][:].rearrange("p (a i t) -> p a t i", i=4, t=PACK)
             src = y[c][:].rearrange("p t (a i) -> p a t i", i=4)
             if on_vector:
@@ -136,23 +159,26 @@ def tile_picked_zfilm_silu_po_kernel(tc, x_words, x_scales, w1, w2, feat, offs, 
         def store_words(a, b):
             nc.sync.dma_start(out_words[:, PACK * a : PACK * b].bitcast(I32), y_codes[:, a:b].bitcast(I32))
 
-        modulate(0)
-        modulate(1)
+        plus_one(1, "g11")
+        plus_one(3, "w2_raw")
+        modulate(0, "wb10")
+        modulate_gpsimd(1, "wb11")
         shift(0)
-        round_y(0, False)
+        modulate(2, "v2")
+        modulate_gpsimd(3, "v3")
+        round_y(0, False, "yb0")
         shift(1)
-        round_y(1, False)
-        modulate(2)
-        modulate(3)
-        quantise_y(0)
         shift(2)
         shift(3)
+        y_codes = keep.tile([P, S], U32, name="y_codes", tag="w2_raw", align_bytes=64)
+        round_y(2, False, "u3")
+        round_y(1, True, "v3")
+        quantise_y(0)
+        round_y(3, True, "yb3")
         quantise_y(1)
         store_words(0, HALF)
-        round_y(2, True)
-        quantise_y(2)
-        round_y(3, True)
         quantise_y(3)
+        quantise_y(2)
         store_words(HALF, S)
         for q in range(4):
             eng = nc.scalar if q % 2 == 0 else nc.sync

@@ -30,13 +30,14 @@ def tile_picked_zfilm_silu_po_kernel(tc, x_words, x_scales, w1, w2, feat, offs, 
         keep = ctx.enter_context(tc.tile_pool(name="keep", bufs=1))
         psum = ctx.enter_context(tc.psum_pool(name="psum", bufs=1))
 
-        offsets = keep.tile([P, S // 16], U16, name="offsets")
-        nc.sync.dma_start(offsets[:], offs)
-        staged_scales = keep.tile([P, T], U8, name="staged_scales", align_bytes=64)
-        for q in range(4):
-            nc.scalar.dma_start(staged_scales[32 * q : 32 * q + 4, :].bitcast(I32), x_scales[0, 4 * q : 4 * q + 4, :].bitcast(I32))
         w1_raw = keep.tile([P, PACK, N], F32, name="w1_raw")
         nc.sync.dma_start(w1_raw[:], w1.rearrange("(p j) c -> p j c", j=PACK))
+        offsets = keep.tile([P, S // 16], U16, name="offsets")
+        nc.sync.dma_start(offsets[:], offs)
+        table_scales = keep.tile([P, T], U8, name="table_scales", align_bytes=64)
+        nc.vector.memset(table_scales[:].bitcast(I32), 0)
+        for q in range(4):
+            nc.sync.dma_start(table_scales[32 * q : 32 * q + 4, :].bitcast(I32), x_scales[0, 4 * q : 4 * q + 4, :].bitcast(I32))
         table_words = keep.tile([P, T], U32, name="table_words", align_bytes=64)
         nc.sync.dma_start(table_words[:].bitcast(I32), x_words[0].rearrange("p n t -> p (n t)").bitcast(I32))
         w2_raw = keep.tile([P, PACK, N], F32, name="w2_raw", tag="w2_raw", align_bytes=64)
@@ -48,10 +49,6 @@ def tile_picked_zfilm_silu_po_kernel(tc, x_words, x_scales, w1, w2, feat, offs, 
             nc.sync.dma_start(f[:], feat_rows[:, :, h * HALF : (h + 1) * HALF])
             feat_sb.append(f)
 
-        table_scales = keep.tile([P, T], U8, name="table_scales", align_bytes=64)
-        nc.vector.memset(table_scales[:].bitcast(I32), 0)
-        for q in range(4):
-            nc.vector.tensor_copy(table_scales[32 * q : 32 * q + 4, :].bitcast(I32), staged_scales[32 * q : 32 * q + 4, :].bitcast(I32))
         x_sc = keep.tile([P, S], U8, name="x_sc", align_bytes=64)
         nc.vector.tensor_copy(x_sc[:], table_scales[:].indirect(offsets[:]))
 
@@ -104,9 +101,9 @@ def tile_picked_zfilm_silu_po_kernel(tc, x_words, x_scales, w1, w2, feat, offs, 
             return bank
 
         g = {}
-        for c in (1, 0, 3, 2):
+        for c in range(NCH):
             g[c] = product(0, c)
-        round_w(1, w2_raw, 84)
+        round_w(1, w2_raw, 128)
         quantise_w(1)
 
         y_scales = keep.tile([P, S], U8, name="y_scales", align_bytes=64)
@@ -159,26 +156,24 @@ def tile_picked_zfilm_silu_po_kernel(tc, x_words, x_scales, w1, w2, feat, offs, 
         def store_words(a, b):
             nc.sync.dma_start(out_words[:, PACK * a : PACK * b].bitcast(I32), y_codes[:, a:b].bitcast(I32))
 
-        plus_one(1, "g11")
-        plus_one(3, "w2_raw")
-        modulate(0, "wb10")
-        modulate_gpsimd(1, "wb11")
+        modulate(0, "v0")
+        modulate(1, "v1")
         shift(0)
-        modulate(2, "v2")
-        modulate_gpsimd(3, "v3")
         round_y(0, False, "yb0")
         shift(1)
+        round_y(1, False, "yb1")
+        modulate(2, "v2")
+        modulate(3, "v3")
         shift(2)
         shift(3)
-        y_codes = keep.tile([P, S], U32, name="y_codes", tag="w2_raw", align_bytes=64)
-        round_y(2, False, "u3")
-        round_y(1, True, "v3")
+        y_codes = keep.tile([P, S], U32, name="y_codes", tag="v3", align_bytes=64)
+        round_y(2, True, "yb2")
         quantise_y(0)
-        round_y(3, True, "yb3")
         quantise_y(1)
         store_words(0, HALF)
-        quantise_y(3)
+        round_y(3, True, "yb3")
         quantise_y(2)
+        quantise_y(3)
         store_words(HALF, S)
         for q in range(4):
             eng = nc.scalar if q % 2 == 0 else nc.sync

@@ -60,12 +60,12 @@ def tile_picked_zfilm_silu_po_kernel(tc, x_words, x_scales, w1, w2, feat, offs, 
                 rounded[i, u] = keep.tile([P, 2 * P * PACK], BF16, name="wb%d%d" % (i, u), tag="wb%d%d" % (i, u), align_bytes=64)
 
         def round_w(i, raw, split):
-            dealt = raw[:].rearrange("p j (m t) -> p m t j", t=PACK)
-            dst = [rounded[i, u][:].rearrange("p (t m j) -> p m t j", t=2, j=PACK) for u in range(2)]
+            dealt = raw[:].rearrange("p j (m t) -> p m j t", t=PACK)
+            dst = [rounded[i, u][:].rearrange("p (t m j) -> p m j t", t=2, j=PACK) for u in range(2)]
             if split < P:
-                nc.vector.tensor_copy(dst[1][:, split:], dealt[:, split:, 2:4, :])
-            nc.scalar.copy(dst[1][:, :split], dealt[:, :split, 2:4, :])
-            nc.vector.tensor_copy(dst[0], dealt[:, :, 0:2, :])
+                nc.vector.tensor_copy(dst[1][:, split:], dealt[:, split:, :, 2:4])
+            nc.scalar.copy(dst[1][:, :split], dealt[:, :split, :, 2:4])
+            nc.vector.tensor_copy(dst[0], dealt[:, :, :, 0:2])
 
         def quantise_w(i):
             for u in range(2):

@@ -14,7 +14,6 @@ U8 = mybir.dt.uint8
 FP8X4 = mybir.dt.float8_e4m3fn_x4
 ADD = mybir.AluOpType.add
 MULT = mybir.AluOpType.mult
-COPY = mybir.ActivationFunctionType.Copy
 SILU = mybir.ActivationFunctionType.Silu
 
 P = 128
@@ -30,8 +29,12 @@ def tile_picked_zfilm_silu_po_kernel(tc, x_words, x_scales, w1, w2, feat, offs, 
         keep = ctx.enter_context(tc.tile_pool(name="keep", bufs=1))
         psum = ctx.enter_context(tc.psum_pool(name="psum", bufs=1))
 
-        w1_raw = keep.tile([P, PACK, N], F32, name="w1_raw")
-        nc.sync.dma_start(w1_raw[:], w1.rearrange("(p j) c -> p j c", j=PACK))
+        def load_columns(src, a, b, name):
+            tile = keep.tile([P, PACK, b - a], F32, name=name, align_bytes=64)
+            nc.sync.dma_start(tile[:], src.rearrange("(p j) c -> p j c", j=PACK)[:, :, a:b])
+            return tile
+
+        w1_raw = load_columns(w1, 0, N, "w1_raw")
         offsets = keep.tile([P, S // 16], U16, name="offsets")
         nc.sync.dma_start(offsets[:], offs)
         table_scales = keep.tile([P, T], U8, name="table_scales", align_bytes=64)
@@ -40,43 +43,47 @@ def tile_picked_zfilm_silu_po_kernel(tc, x_words, x_scales, w1, w2, feat, offs, 
             nc.sync.dma_start(table_scales[32 * q : 32 * q + 4, :].bitcast(I32), x_scales[0, 4 * q : 4 * q + 4, :].bitcast(I32))
         table_words = keep.tile([P, T], U32, name="table_words", align_bytes=64)
         nc.sync.dma_start(table_words[:].bitcast(I32), x_words[0].rearrange("p n t -> p (n t)").bitcast(I32))
-        w2_raw = keep.tile([P, PACK, N], F32, name="w2_raw", tag="w2_raw", align_bytes=64)
-        nc.sync.dma_start(w2_raw[:], w2.rearrange("(p j) c -> p j c", j=PACK))
-        feat_rows = feat.rearrange("(p t) s -> p t s", t=PACK)
-        feat_sb = []
-        for h in range(2):
-            f = keep.tile([P, PACK, HALF], F32, name="feat%d" % h)
-            nc.sync.dma_start(f[:], feat_rows[:, :, h * HALF : (h + 1) * HALF])
-            feat_sb.append(f)
+        w2_raw = [load_columns(w2, h * (N // 2), (h + 1) * (N // 2), "w2_raw%d" % h) for h in range(2)]
+        feat_cuts = [0, CH, 2 * CH, S]
+        feat_sb = [load_columns(feat, a, b, "feat%d" % a) for a, b in zip(feat_cuts, feat_cuts[1:])]
+
+        warm = keep.tile([P, 1], F32, name="warm")
+        nc.scalar.activation(warm[:], w1_raw[:, 0, 0:1], SILU)
 
         x_sc = keep.tile([P, S], U8, name="x_sc", align_bytes=64)
         nc.vector.tensor_copy(x_sc[:], table_scales[:].indirect(offsets[:]))
 
-        rounded = {}
         w_codes = {}
         w_scales = {}
         for i in range(2):
             for u in range(2):
-                rounded[i, u] = keep.tile([P, 2 * P * PACK], BF16, name="wb%d%d" % (i, u), tag="wb%d%d" % (i, u), align_bytes=64)
+                w_codes[i, u] = keep.tile([P, 2, P], U32, name="wc%d%d" % (i, u), align_bytes=64)
+                w_scales[i, u] = keep.tile([P, 2, P], U8, name="ws%d%d" % (i, u), align_bytes=64)
 
-        def round_w(i, raw, split):
+        def quantise_w(i, raw, m0, m1):
+            width = m1 - m0
             dealt = raw[:].rearrange("p j (m t) -> p m j t", t=PACK)
-            dst = [rounded[i, u][:].rearrange("p (t m j) -> p m j t", t=2, j=PACK) for u in range(2)]
-            if split < P:
-                nc.vector.tensor_copy(dst[1][:, split:], dealt[:, split:, :, 2:4])
-            nc.scalar.copy(dst[1][:, :split], dealt[:, :split, :, 2:4])
-            nc.vector.tensor_copy(dst[0], dealt[:, :, :, 0:2])
-
-        def quantise_w(i):
+            rounded = []
             for u in range(2):
-                codes = keep.tile([P, 2 * P], U32, name="wc%d%d" % (i, u), align_bytes=64)
-                scales = keep.tile([P, 2 * P], U8, name="ws%d%d" % (i, u), align_bytes=64)
-                nc.vector.quantize_mx(out=codes[:].bitcast(FP8X4), scales=scales[:], in_=rounded[i, u][:])
-                w_codes[2 * i + u] = codes
-                w_scales[2 * i + u] = scales
+                r = keep.tile([P, 2, width * PACK], BF16, name="wb%d%d_%d" % (i, u, m0), align_bytes=64)
+                dst = r[:].rearrange("p t (m j) -> p m j t", j=PACK)
+                if u == 0:
+                    nc.vector.tensor_copy(dst, dealt[:, :, :, 0:2])
+                else:
+                    nc.scalar.copy(dst, dealt[:, :, :, 2:4])
+                rounded.append(r)
+            for u in range(2):
+                if width == P:
+                    nc.vector.quantize_mx(
+                        out=w_codes[i, u][:].rearrange("p e m -> p (e m)").bitcast(FP8X4),
+                        scales=w_scales[i, u][:].rearrange("p e m -> p (e m)"),
+                        in_=rounded[u][:].rearrange("p e c -> p (e c)"),
+                    )
+                else:
+                    for e in range(2):
+                        nc.vector.quantize_mx(out=w_codes[i, u][:, e, m0:m1].bitcast(FP8X4), scales=w_scales[i, u][:, e, m0:m1], in_=rounded[u][:, e, :])
 
-        round_w(0, w1_raw, P)
-        quantise_w(0)
+        quantise_w(0, w1_raw, 0, P)
 
         x_codes = []
         for h in range(2):
@@ -91,8 +98,8 @@ def tile_picked_zfilm_silu_po_kernel(tc, x_words, x_scales, w1, w2, feat, offs, 
                 u, e = divmod(t, 2)
                 nc.tensor.matmul_mx(
                     out=bank[:, t, :],
-                    lhsT=w_codes[2 * i + u][:, e * P : (e + 1) * P].bitcast(FP8X4),
-                    lhsT_scale=w_scales[2 * i + u][:, e * P : (e + 1) * P],
+                    lhsT=w_codes[i, u][:, e, :].bitcast(FP8X4),
+                    lhsT_scale=w_scales[i, u][:, e, :],
                     rhs=x_codes[h][:, o : o + CH].bitcast(FP8X4),
                     rhs_scale=x_sc[:, c * CH : (c + 1) * CH],
                     start=True,
@@ -100,81 +107,66 @@ def tile_picked_zfilm_silu_po_kernel(tc, x_words, x_scales, w1, w2, feat, offs, 
                 )
             return bank
 
-        g = {}
-        for c in range(NCH):
-            g[c] = product(0, c)
-        round_w(1, w2_raw, 128)
-        quantise_w(1)
+        g = [product(0, c) for c in range(NCH)]
+        for h in range(2):
+            quantise_w(1, w2_raw[h], h * (P // 2), (h + 1) * (P // 2))
+        hb = [product(1, c) for c in range(NCH)]
 
         y_scales = keep.tile([P, S], U8, name="y_scales", align_bytes=64)
         out_rows = out_0.rearrange("(p t) s -> p t s", t=PACK)
         out_words = out_1[0].rearrange("p n t -> p (n t)")
 
-        v = {}
-        g1 = {}
-        u_sb = {}
-        y = {}
-        yb = {}
-
         def feat_of(c):
-            h, o = divmod(c * CH, HALF)
-            return feat_sb[h][:, :, o : o + CH]
+            k = min(c, len(feat_sb) - 1)
+            o = c * CH - feat_cuts[k]
+            return feat_sb[k][:, :, o : o + CH]
 
-        def modulate(c, tag):
-            v[c] = keep.tile([P, PACK, CH], F32, name="v%d" % c, tag=tag, align_bytes=64)
+        v = {}
+        y = {}
+        yb_first = keep.tile([P, 2, CH * PACK], BF16, name="yb_first", align_bytes=64)
+        yb_last = [keep.tile([P, CH * PACK], BF16, name="yb%d" % c, align_bytes=64) for c in range(2)]
+
+        def round_y(c):
+            src = y[c][:].rearrange("p t (a i) -> p a t i", i=4)
+            if c < 2:
+                nc.scalar.copy(yb_first[:, c, :].rearrange("p (a i t) -> p a t i", i=4, t=PACK), src)
+            else:
+                nc.vector.tensor_copy(yb_last[c - 2][:].rearrange("p (a i t) -> p a t i", i=4, t=PACK), src)
+
+        def modulate(c):
+            v[c] = keep.tile([P, PACK, CH], F32, name="v%d" % c, tag="v%d" % (c % 2), align_bytes=64)
             nc.vector.scalar_tensor_tensor(v[c][:], g[c][:], 1.0, feat_of(c), ADD, MULT)
 
-        def plus_one(c, tag):
-            g1[c] = keep.tile([P, PACK, CH], F32, name="g1%d" % c, tag=tag, align_bytes=64)
-            nc.scalar.activation(g1[c][:], g[c][:], COPY, bias=1.0)
-
-        def modulate_gpsimd(c, tag):
-            v[c] = keep.tile([P, PACK, CH], F32, name="v%d" % c, tag=tag, align_bytes=64)
-            nc.gpsimd.tensor_tensor(v[c][:], g1[c][:], feat_of(c), MULT)
-
         def shift(c):
-            hb = product(1, c)
-            u_sb[c] = keep.tile([P, PACK, CH], F32, name="u%d" % c, tag="u%d" % c, align_bytes=64)
-            nc.vector.tensor_tensor(u_sb[c][:], hb[:], v[c][:], ADD)
+            u_sb = keep.tile([P, PACK, CH], F32, name="u%d" % c, align_bytes=64)
+            nc.vector.tensor_tensor(u_sb[:], hb[c][:], v[c][:], ADD)
             y[c] = keep.tile([P, PACK, CH], F32, name="y%d" % c)
-            nc.scalar.activation(y[c][:], u_sb[c][:], SILU)
+            nc.scalar.activation(y[c][:], u_sb[:], SILU)
             nc.sync.dma_start(out_rows[:, :, c * CH : (c + 1) * CH], y[c][:])
 
-        def round_y(c, on_vector, tag):
-            yb[c] = keep.tile([P, CH * PACK], BF16, name="yb%d" % c, tag=tag, align_bytes=64)
-            dst = yb[c][:].rearrange("p (a i t) -> p a t i", i=4, t=PACK)
-            src = y[c][:].rearrange("p t (a i) -> p a t i", i=4)
-            if on_vector:
-                nc.vector.tensor_copy(dst, src)
-            else:
-                nc.scalar.copy(dst, src)
+        modulate(0)
+        for c in range(NCH):
+            if c + 1 < NCH:
+                modulate(c + 1)
+            shift(c)
+            if c < 2:
+                round_y(c)
 
-        def quantise_y(c):
-            cols = slice(c * CH, (c + 1) * CH)
-            nc.vector.quantize_mx(out=y_codes[:, cols].bitcast(FP8X4), scales=y_scales[:, cols], in_=yb[c][:])
+        y_codes = keep.tile([P, S], U32, name="y_codes", tag="v1", align_bytes=64)
+
+        def quantise_y(a, b, src):
+            nc.vector.quantize_mx(out=y_codes[:, a:b].bitcast(FP8X4), scales=y_scales[:, a:b], in_=src)
 
         def store_words(a, b):
             nc.sync.dma_start(out_words[:, PACK * a : PACK * b].bitcast(I32), y_codes[:, a:b].bitcast(I32))
 
-        modulate(0, "v0")
-        modulate(1, "v1")
-        shift(0)
-        round_y(0, False, "yb0")
-        shift(1)
-        round_y(1, False, "yb1")
-        modulate(2, "v2")
-        modulate(3, "v3")
-        shift(2)
-        shift(3)
-        y_codes = keep.tile([P, S], U32, name="y_codes", tag="v3", align_bytes=64)
-        round_y(2, True, "yb2")
-        quantise_y(0)
-        quantise_y(1)
-        store_words(0, HALF)
-        round_y(3, True, "yb3")
-        quantise_y(2)
-        quantise_y(3)
-        store_words(HALF, S)
+        quantise_y(0, HALF, yb_first[:].rearrange("p c n -> p (c n)"))
+        round_y(2)
+        quantise_y(2 * CH, 3 * CH, yb_last[0][:])
+        store_words(0, S - CH)
+        round_y(3)
+        quantise_y(3 * CH, S, yb_last[1][:])
+        store_words(S - CH, S)
         for q in range(4):
             eng = nc.scalar if q % 2 == 0 else nc.sync
             eng.dma_start(out_2[0, 4 * q : 4 * q + 4, :].bitcast(I32), y_scales[32 * q : 32 * q + 4, :].bitcast(I32))

@@ -14,6 +14,7 @@ U8 = mybir.dt.uint8
 FP8X4 = mybir.dt.float8_e4m3fn_x4
 ADD = mybir.AluOpType.add
 MULT = mybir.AluOpType.mult
+COPY = mybir.ActivationFunctionType.Copy
 SILU = mybir.ActivationFunctionType.Silu
 
 P = 128
@@ -30,7 +31,7 @@ def tile_picked_zfilm_silu_po_kernel(tc, x_words, x_scales, w1, w2, feat, offs, 
         psum = ctx.enter_context(tc.psum_pool(name="psum", bufs=1))
 
         def load_columns(src, a, b, name):
-            tile = keep.tile([P, PACK, b - a], F32, name=name, align_bytes=64)
+            tile = keep.tile([P, PACK, b - a], F32, name=name, tag=name, align_bytes=64)
             nc.sync.dma_start(tile[:], src.rearrange("(p j) c -> p j c", j=PACK)[:, :, a:b])
             return tile
 
@@ -43,8 +44,9 @@ def tile_picked_zfilm_silu_po_kernel(tc, x_words, x_scales, w1, w2, feat, offs, 
             nc.sync.dma_start(table_scales[32 * q : 32 * q + 4, :].bitcast(I32), x_scales[0, 4 * q : 4 * q + 4, :].bitcast(I32))
         table_words = keep.tile([P, T], U32, name="table_words", align_bytes=64)
         nc.sync.dma_start(table_words[:].bitcast(I32), x_words[0].rearrange("p n t -> p (n t)").bitcast(I32))
-        w2_raw = [load_columns(w2, h * (N // 2), (h + 1) * (N // 2), "w2_raw%d" % h) for h in range(2)]
-        feat_cuts = [0, CH, 2 * CH, S]
+        w2_cuts = [0, N // 2, 3 * N // 4, N]
+        w2_raw = [load_columns(w2, a, b, "w2_raw%d" % a) for a, b in zip(w2_cuts, w2_cuts[1:])]
+        feat_cuts = [c * CH for c in range(NCH + 1)]
         feat_sb = [load_columns(feat, a, b, "feat%d" % a) for a, b in zip(feat_cuts, feat_cuts[1:])]
 
         warm = keep.tile([P, 1], F32, name="warm")
@@ -60,30 +62,21 @@ def tile_picked_zfilm_silu_po_kernel(tc, x_words, x_scales, w1, w2, feat, offs, 
                 w_codes[i, u] = keep.tile([P, 2, P], U32, name="wc%d%d" % (i, u), align_bytes=64)
                 w_scales[i, u] = keep.tile([P, 2, P], U8, name="ws%d%d" % (i, u), align_bytes=64)
 
-        def quantise_w(i, raw, m0, m1):
-            width = m1 - m0
-            dealt = raw[:].rearrange("p j (m t) -> p m j t", t=PACK)
-            rounded = []
+        def quantise_w(i, raws, cuts):
+            rounded = [keep.tile([P, 2, P * PACK], BF16, name="wb%d%d" % (i, u), align_bytes=64) for u in range(2)]
+            for raw, a, b in zip(raws, cuts, cuts[1:]):
+                dealt = raw[:].rearrange("p j (m t) -> p m j t", t=PACK)
+                dst = [r[:].rearrange("p t (m j) -> p m j t", j=PACK)[:, a // PACK : b // PACK] for r in rounded]
+                nc.vector.tensor_copy(dst[0], dealt[:, :, :, 0:2])
+                nc.scalar.copy(dst[1], dealt[:, :, :, 2:4])
             for u in range(2):
-                r = keep.tile([P, 2, width * PACK], BF16, name="wb%d%d_%d" % (i, u, m0), align_bytes=64)
-                dst = r[:].rearrange("p t (m j) -> p m j t", j=PACK)
-                if u == 0:
-                    nc.vector.tensor_copy(dst, dealt[:, :, :, 0:2])
-                else:
-                    nc.scalar.copy(dst, dealt[:, :, :, 2:4])
-                rounded.append(r)
-            for u in range(2):
-                if width == P:
-                    nc.vector.quantize_mx(
-                        out=w_codes[i, u][:].rearrange("p e m -> p (e m)").bitcast(FP8X4),
-                        scales=w_scales[i, u][:].rearrange("p e m -> p (e m)"),
-                        in_=rounded[u][:].rearrange("p e c -> p (e c)"),
-                    )
-                else:
-                    for e in range(2):
-                        nc.vector.quantize_mx(out=w_codes[i, u][:, e, m0:m1].bitcast(FP8X4), scales=w_scales[i, u][:, e, m0:m1], in_=rounded[u][:, e, :])
+                nc.vector.quantize_mx(
+                    out=w_codes[i, u][:].rearrange("p e m -> p (e m)").bitcast(FP8X4),
+                    scales=w_scales[i, u][:].rearrange("p e m -> p (e m)"),
+                    in_=rounded[u][:].rearrange("p e c -> p (e c)"),
+                )
 
-        quantise_w(0, w1_raw, 0, P)
+        quantise_w(0, [w1_raw], [0, N])
 
         x_codes = []
         for h in range(2):
@@ -108,65 +101,70 @@ def tile_picked_zfilm_silu_po_kernel(tc, x_words, x_scales, w1, w2, feat, offs, 
             return bank
 
         g = [product(0, c) for c in range(NCH)]
-        for h in range(2):
-            quantise_w(1, w2_raw[h], h * (P // 2), (h + 1) * (P // 2))
+        quantise_w(1, w2_raw, w2_cuts)
         hb = [product(1, c) for c in range(NCH)]
 
         y_scales = keep.tile([P, S], U8, name="y_scales", align_bytes=64)
         out_rows = out_0.rearrange("(p t) s -> p t s", t=PACK)
         out_words = out_1[0].rearrange("p n t -> p (n t)")
 
-        def feat_of(c):
-            k = min(c, len(feat_sb) - 1)
-            o = c * CH - feat_cuts[k]
-            return feat_sb[k][:, :, o : o + CH]
-
         v = {}
+        u_sb = {}
         y = {}
-        yb_first = keep.tile([P, 2, CH * PACK], BF16, name="yb_first", align_bytes=64)
-        yb_last = [keep.tile([P, CH * PACK], BF16, name="yb%d" % c, align_bytes=64) for c in range(2)]
 
-        def round_y(c):
-            src = y[c][:].rearrange("p t (a i) -> p a t i", i=4)
-            if c < 2:
-                nc.scalar.copy(yb_first[:, c, :].rearrange("p (a i t) -> p a t i", i=4, t=PACK), src)
-            else:
-                nc.vector.tensor_copy(yb_last[c - 2][:].rearrange("p (a i t) -> p a t i", i=4, t=PACK), src)
+        def interleaved(ap):
+            return ap.rearrange("p (a i t) -> p a t i", i=4, t=PACK)
+
+        def by_fours(tile):
+            return tile[:].rearrange("p t (a i) -> p a t i", i=4)
 
         def modulate(c):
-            v[c] = keep.tile([P, PACK, CH], F32, name="v%d" % c, tag="v%d" % (c % 2), align_bytes=64)
-            nc.vector.scalar_tensor_tensor(v[c][:], g[c][:], 1.0, feat_of(c), ADD, MULT)
+            v[c] = keep.tile([P, PACK, CH], F32, name="v%d" % c, tag="v%d" % (c % 3), align_bytes=64)
+            nc.vector.scalar_tensor_tensor(v[c][:], g[c][:], 1.0, feat_sb[c][:], ADD, MULT)
 
-        def shift(c):
-            u_sb = keep.tile([P, PACK, CH], F32, name="u%d" % c, align_bytes=64)
-            nc.vector.tensor_tensor(u_sb[:], hb[c][:], v[c][:], ADD)
+        def shift(c, tag):
+            u_sb[c] = keep.tile([P, PACK, CH], F32, name="u%d" % c, tag=tag, align_bytes=64)
+            nc.vector.tensor_tensor(u_sb[c][:], hb[c][:], v[c][:], ADD)
             y[c] = keep.tile([P, PACK, CH], F32, name="y%d" % c)
-            nc.scalar.activation(y[c][:], u_sb[:], SILU)
+            nc.scalar.activation(y[c][:], u_sb[c][:], SILU)
             nc.sync.dma_start(out_rows[:, :, c * CH : (c + 1) * CH], y[c][:])
 
+        g1 = keep.tile([P, PACK, CH], F32, name="g1", tag="w2_raw384", align_bytes=64)
+        nc.scalar.activation(g1[:], g[2][:], COPY, bias=1.0)
+        v[2] = keep.tile([P, PACK, CH], F32, name="v2", align_bytes=64)
+        nc.gpsimd.tensor_tensor(v[2][:], g1[:], feat_sb[2][:], MULT)
+
+        yb0 = keep.tile([P, CH * PACK], BF16, name="yb0", align_bytes=64)
         modulate(0)
-        for c in range(NCH):
-            if c + 1 < NCH:
-                modulate(c + 1)
-            shift(c)
-            if c < 2:
-                round_y(c)
+        modulate(1)
+        shift(0, "u0")
+        nc.scalar.activation(interleaved(yb0[:]), by_fours(u_sb[0]), SILU)
+        modulate(3)
+        shift(1, "u1")
+        shift(2, "u2")
+        shift(3, "u3")
 
-        y_codes = keep.tile([P, S], U32, name="y_codes", tag="v1", align_bytes=64)
+        yb1 = keep.tile([P, CH * PACK], BF16, name="yb1", tag="v0", align_bytes=64)
+        yb2 = keep.tile([P, CH * PACK], BF16, name="yb2", align_bytes=64)
+        yb3 = keep.tile([P, CH * PACK], BF16, name="yb3", align_bytes=64)
+        y_codes = keep.tile([P, S], U32, name="y_codes", align_bytes=64)
+        nc.scalar.activation(interleaved(yb3[:]), by_fours(u_sb[3]), SILU)
 
-        def quantise_y(a, b, src):
-            nc.vector.quantize_mx(out=y_codes[:, a:b].bitcast(FP8X4), scales=y_scales[:, a:b], in_=src)
+        def quantise_y(c, src):
+            cols = slice(c * CH, (c + 1) * CH)
+            nc.vector.quantize_mx(out=y_codes[:, cols].bitcast(FP8X4), scales=y_scales[:, cols], in_=src[:])
 
         def store_words(a, b):
             nc.sync.dma_start(out_words[:, PACK * a : PACK * b].bitcast(I32), y_codes[:, a:b].bitcast(I32))
 
-        quantise_y(0, HALF, yb_first[:].rearrange("p c n -> p (c n)"))
-        round_y(2)
-        quantise_y(2 * CH, 3 * CH, yb_last[0][:])
-        store_words(0, S - CH)
-        round_y(3)
-        quantise_y(3 * CH, S, yb_last[1][:])
-        store_words(S - CH, S)
+        quantise_y(0, yb0)
+        nc.vector.tensor_copy(interleaved(yb1[:]), by_fours(y[1]))
+        nc.vector.tensor_copy(interleaved(yb2[:]), by_fours(y[2]))
+        quantise_y(1, yb1)
+        quantise_y(2, yb2)
+        store_words(0, 3 * CH)
+        quantise_y(3, yb3)
+        store_words(3 * CH, S)
         for q in range(4):
             eng = nc.scalar if q % 2 == 0 else nc.sync
             eng.dma_start(out_2[0, 4 * q : 4 * q + 4, :].bitcast(I32), y_scales[32 * q : 32 * q + 4, :].bitcast(I32))

@@ -44,10 +44,15 @@ def tile_picked_zfilm_silu_po_kernel(tc, x_words, x_scales, w1, w2, feat, offs, 
             nc.sync.dma_start(table_scales[32 * q : 32 * q + 4, :].bitcast(I32), x_scales[0, 4 * q : 4 * q + 4, :].bitcast(I32))
         table_words = keep.tile([P, T], U32, name="table_words", align_bytes=64)
         nc.sync.dma_start(table_words[:].bitcast(I32), x_words[0].rearrange("p n t -> p (n t)").bitcast(I32))
-        w2_cuts = [0, N // 2, 3 * N // 4, N]
+        w2_cuts = [0, N // 2, N]
         w2_raw = [load_columns(w2, a, b, "w2_raw%d" % a) for a, b in zip(w2_cuts, w2_cuts[1:])]
-        feat_cuts = [c * CH for c in range(NCH + 1)]
-        feat_sb = [load_columns(feat, a, b, "feat%d" % a) for a, b in zip(feat_cuts, feat_cuts[1:])]
+        feat_rows = feat.rearrange("(p t) s -> p t s", t=PACK)
+        feat_sb = []
+        for c in range(NCH):
+            h, u = divmod(c, 2)
+            f = keep.tile([P, 2, HALF], F32, name="feat%d" % c, align_bytes=64)
+            nc.sync.dma_start(f[:], feat_rows[:, 2 * u : 2 * u + 2, h * HALF : (h + 1) * HALF])
+            feat_sb.append(f)
 
         warm = keep.tile([P, 1], F32, name="warm")
         nc.scalar.activation(warm[:], w1_raw[:, 0, 0:1], SILU)
@@ -85,16 +90,15 @@ def tile_picked_zfilm_silu_po_kernel(tc, x_words, x_scales, w1, w2, feat, offs, 
             x_codes.append(xc)
 
         def product(i, c):
-            bank = psum.tile([P, PACK, CH], F32, name="bank%d%d" % (i, c))
-            h, o = divmod(c * CH, HALF)
-            for t in range(PACK):
-                u, e = divmod(t, 2)
+            bank = psum.tile([P, 2, HALF], F32, name="bank%d%d" % (i, c))
+            h, u = divmod(c, 2)
+            for e in range(2):
                 nc.tensor.matmul_mx(
-                    out=bank[:, t, :],
+                    out=bank[:, e, :],
                     lhsT=w_codes[i, u][:, e, :].bitcast(FP8X4),
                     lhsT_scale=w_scales[i, u][:, e, :],
-                    rhs=x_codes[h][:, o : o + CH].bitcast(FP8X4),
-                    rhs_scale=x_sc[:, c * CH : (c + 1) * CH],
+                    rhs=x_codes[h][:].bitcast(FP8X4),
+                    rhs_scale=x_sc[:, h * HALF : (h + 1) * HALF],
                     start=True,
                     stop=True,
                 )
@@ -109,46 +113,46 @@ def tile_picked_zfilm_silu_po_kernel(tc, x_words, x_scales, w1, w2, feat, offs, 
         out_words = out_1[0].rearrange("p n t -> p (n t)")
 
         v = {}
-        u_sb = {}
-        y = {}
+        u_sb = [keep.tile([P, PACK, HALF], F32, name="u%d" % h, align_bytes=64) for h in range(2)]
+        y = [keep.tile([P, PACK, HALF], F32, name="y%d" % h, align_bytes=64) for h in range(2)]
 
         def interleaved(ap):
             return ap.rearrange("p (a i t) -> p a t i", i=4, t=PACK)
 
-        def by_fours(tile):
-            return tile[:].rearrange("p t (a i) -> p a t i", i=4)
+        def by_fours(tile, k):
+            return tile[:, :, k * CH : (k + 1) * CH].rearrange("p t (a i) -> p a t i", i=4)
 
         def modulate(c):
-            v[c] = keep.tile([P, PACK, CH], F32, name="v%d" % c, tag="v%d" % (c % 3), align_bytes=64)
+            v[c] = keep.tile([P, 2, HALF], F32, name="v%d" % c, tag="v%d" % (c % 3), align_bytes=64)
             nc.vector.scalar_tensor_tensor(v[c][:], g[c][:], 1.0, feat_sb[c][:], ADD, MULT)
 
-        def shift(c, tag):
-            u_sb[c] = keep.tile([P, PACK, CH], F32, name="u%d" % c, tag=tag, align_bytes=64)
-            nc.vector.tensor_tensor(u_sb[c][:], hb[c][:], v[c][:], ADD)
-            y[c] = keep.tile([P, PACK, CH], F32, name="y%d" % c)
-            nc.scalar.activation(y[c][:], u_sb[c][:], SILU)
-            nc.sync.dma_start(out_rows[:, :, c * CH : (c + 1) * CH], y[c][:])
+        def shift(c):
+            h, u = divmod(c, 2)
+            rows = slice(2 * u, 2 * u + 2)
+            nc.vector.tensor_tensor(u_sb[h][:, rows, :], hb[c][:], v[c][:], ADD)
+            nc.scalar.activation(y[h][:, rows, :], u_sb[h][:, rows, :], SILU)
+            nc.sync.dma_start(out_rows[:, rows, h * HALF : (h + 1) * HALF], y[h][:, rows, :])
 
-        g1 = keep.tile([P, PACK, CH], F32, name="g1", tag="w2_raw384", align_bytes=64)
+        g1 = keep.tile([P, 2, HALF], F32, name="g1", tag="w2_raw256", align_bytes=64)
         nc.scalar.activation(g1[:], g[2][:], COPY, bias=1.0)
-        v[2] = keep.tile([P, PACK, CH], F32, name="v2", align_bytes=64)
+        v[2] = keep.tile([P, 2, HALF], F32, name="v2", align_bytes=64)
         nc.gpsimd.tensor_tensor(v[2][:], g1[:], feat_sb[2][:], MULT)
 
         yb0 = keep.tile([P, CH * PACK], BF16, name="yb0", align_bytes=64)
         modulate(0)
         modulate(1)
-        shift(0, "u0")
-        nc.scalar.activation(interleaved(yb0[:]), by_fours(u_sb[0]), SILU)
+        shift(0)
+        shift(1)
+        nc.scalar.activation(interleaved(yb0[:]), by_fours(u_sb[0], 0), SILU)
         modulate(3)
-        shift(1, "u1")
-        shift(2, "u2")
-        shift(3, "u3")
+        shift(2)
+        shift(3)
 
         yb1 = keep.tile([P, CH * PACK], BF16, name="yb1", tag="v0", align_bytes=64)
         yb2 = keep.tile([P, CH * PACK], BF16, name="yb2", align_bytes=64)
         yb3 = keep.tile([P, CH * PACK], BF16, name="yb3", align_bytes=64)
         y_codes = keep.tile([P, S], U32, name="y_codes", align_bytes=64)
-        nc.scalar.activation(interleaved(yb3[:]), by_fours(u_sb[3]), SILU)
+        nc.scalar.activation(interleaved(yb3[:]), by_fours(u_sb[1], 1), SILU)
 
         def quantise_y(c, src):
             cols = slice(c * CH, (c + 1) * CH)
@@ -158,13 +162,13 @@ def tile_picked_zfilm_silu_po_kernel(tc, x_words, x_scales, w1, w2, feat, offs, 
             nc.sync.dma_start(out_words[:, PACK * a : PACK * b].bitcast(I32), y_codes[:, a:b].bitcast(I32))
 
         quantise_y(0, yb0)
-        nc.vector.tensor_copy(interleaved(yb1[:]), by_fours(y[1]))
-        nc.vector.tensor_copy(interleaved(yb2[:]), by_fours(y[2]))
+        nc.vector.tensor_copy(interleaved(yb1[:]), by_fours(y[0], 1))
+        nc.vector.tensor_copy(interleaved(yb2[:]), by_fours(y[1], 0))
         quantise_y(1, yb1)
+        store_words(0, HALF)
         quantise_y(2, yb2)
-        store_words(0, 3 * CH)
         quantise_y(3, yb3)
-        store_words(3 * CH, S)
+        store_words(HALF, S)
         for q in range(4):
             eng = nc.scalar if q % 2 == 0 else nc.sync
             eng.dma_start(out_2[0, 4 * q : 4 * q + 4, :].bitcast(I32), y_scales[32 * q : 32 * q + 4, :].bitcast(I32))

@@ -24,6 +24,10 @@ CH = 128
 NCH = S // CH
 
 
+def chunk(c):
+    return c // 2, 1 - c % 2
+
+
 def tile_picked_zfilm_silu_po_kernel(tc, x_words, x_scales, w1, w2, feat, offs, out_0, out_1, out_2):
     nc = tc.nc
     with ExitStack() as ctx:
@@ -44,13 +48,17 @@ def tile_picked_zfilm_silu_po_kernel(tc, x_words, x_scales, w1, w2, feat, offs, 
             nc.sync.dma_start(table_scales[32 * q : 32 * q + 4, :].bitcast(I32), x_scales[0, 4 * q : 4 * q + 4, :].bitcast(I32))
         table_words = keep.tile([P, T], U32, name="table_words", align_bytes=64)
         nc.sync.dma_start(table_words[:].bitcast(I32), x_words[0].rearrange("p n t -> p (n t)").bitcast(I32))
-        w2_cuts = [0, N // 2, N]
-        w2_raw = [load_columns(w2, a, b, "w2_raw%d" % a) for a, b in zip(w2_cuts, w2_cuts[1:])]
+        w2_rows = w2.rearrange("(p j) c -> p j c", j=PACK)
+        w2_raw = []
+        for k in range(2):
+            raw = keep.tile([P, 2, N], F32, name="w2_raw%d" % k, tag="w2_raw%d" % k, align_bytes=64)
+            nc.sync.dma_start(raw[:], w2_rows[:, 2 * k : 2 * k + 2, :])
+            w2_raw.append(raw)
         feat_rows = feat.rearrange("(p t) s -> p t s", t=PACK)
         feat_sb = []
         for c in range(NCH):
-            h, u = divmod(c, 2)
-            f = keep.tile([P, 2, HALF], F32, name="feat%d" % c, align_bytes=64)
+            h, u = chunk(c)
+            f = keep.tile([P, 2, HALF], F32, name="feat%d" % c, tag="feat%d" % c, align_bytes=64)
             nc.sync.dma_start(f[:], feat_rows[:, 2 * u : 2 * u + 2, h * HALF : (h + 1) * HALF])
             feat_sb.append(f)
 
@@ -62,26 +70,29 @@ def tile_picked_zfilm_silu_po_kernel(tc, x_words, x_scales, w1, w2, feat, offs, 
 
         w_codes = {}
         w_scales = {}
-        for i in range(2):
-            for u in range(2):
-                w_codes[i, u] = keep.tile([P, 2, P], U32, name="wc%d%d" % (i, u), align_bytes=64)
-                w_scales[i, u] = keep.tile([P, 2, P], U8, name="ws%d%d" % (i, u), align_bytes=64)
 
-        def quantise_w(i, raws, cuts):
-            rounded = [keep.tile([P, 2, P * PACK], BF16, name="wb%d%d" % (i, u), align_bytes=64) for u in range(2)]
-            for raw, a, b in zip(raws, cuts, cuts[1:]):
+        def round_w(i, raws):
+            rounded = [keep.tile([P, 2, P * PACK], BF16, name="wb%d%d" % (i, u), tag="wb%d%d" % (i, u), align_bytes=64) for u in range(2)]
+            rows = PACK // len(raws)
+            for k, raw in enumerate(raws):
                 dealt = raw[:].rearrange("p j (m t) -> p m j t", t=PACK)
-                dst = [r[:].rearrange("p t (m j) -> p m j t", j=PACK)[:, a // PACK : b // PACK] for r in rounded]
+                dst = [r[:].rearrange("p t (m j) -> p m j t", j=PACK)[:, :, k * rows : (k + 1) * rows, :] for r in rounded]
                 nc.vector.tensor_copy(dst[0], dealt[:, :, :, 0:2])
                 nc.scalar.copy(dst[1], dealt[:, :, :, 2:4])
-            for u in range(2):
-                nc.vector.quantize_mx(
-                    out=w_codes[i, u][:].rearrange("p e m -> p (e m)").bitcast(FP8X4),
-                    scales=w_scales[i, u][:].rearrange("p e m -> p (e m)"),
-                    in_=rounded[u][:].rearrange("p e c -> p (e c)"),
-                )
+            return rounded
 
-        quantise_w(0, [w1_raw], [0, N])
+        def quantise_w(i, u, rounded, tag):
+            w_codes[i, u] = keep.tile([P, 2, P], U32, name="wc%d%d" % (i, u), tag=tag, align_bytes=64)
+            w_scales[i, u] = keep.tile([P, 2, P], U8, name="ws%d%d" % (i, u), align_bytes=64)
+            nc.vector.quantize_mx(
+                out=w_codes[i, u][:].rearrange("p e m -> p (e m)").bitcast(FP8X4),
+                scales=w_scales[i, u][:].rearrange("p e m -> p (e m)"),
+                in_=rounded[u][:].rearrange("p e c -> p (e c)"),
+            )
+
+        w1_rounded = round_w(0, [w1_raw])
+        for u in range(2):
+            quantise_w(0, u, w1_rounded, "wc0%d" % u)
 
         x_codes = []
         for h in range(2):
@@ -91,7 +102,7 @@ def tile_picked_zfilm_silu_po_kernel(tc, x_words, x_scales, w1, w2, feat, offs, 
 
         def product(i, c):
             bank = psum.tile([P, 2, HALF], F32, name="bank%d%d" % (i, c))
-            h, u = divmod(c, 2)
+            h, u = chunk(c)
             for e in range(2):
                 nc.tensor.matmul_mx(
                     out=bank[:, e, :],
@@ -105,8 +116,7 @@ def tile_picked_zfilm_silu_po_kernel(tc, x_words, x_scales, w1, w2, feat, offs, 
             return bank
 
         g = [product(0, c) for c in range(NCH)]
-        quantise_w(1, w2_raw, w2_cuts)
-        hb = [product(1, c) for c in range(NCH)]
+        w2_rounded = round_w(1, w2_raw)
 
         y_scales = keep.tile([P, S], U8, name="y_scales", align_bytes=64)
         out_rows = out_0.rearrange("(p t) s -> p t s", t=PACK)
@@ -127,19 +137,23 @@ def tile_picked_zfilm_silu_po_kernel(tc, x_words, x_scales, w1, w2, feat, offs, 
             nc.vector.scalar_tensor_tensor(v[c][:], g[c][:], 1.0, feat_sb[c][:], ADD, MULT)
 
         def shift(c):
-            h, u = divmod(c, 2)
+            h, u = chunk(c)
             rows = slice(2 * u, 2 * u + 2)
             nc.vector.tensor_tensor(u_sb[h][:, rows, :], hb[c][:], v[c][:], ADD)
             nc.scalar.activation(y[h][:, rows, :], u_sb[h][:, rows, :], SILU)
             nc.sync.dma_start(out_rows[:, rows, h * HALF : (h + 1) * HALF], y[h][:, rows, :])
 
-        g1 = keep.tile([P, 2, HALF], F32, name="g1", tag="w2_raw256", align_bytes=64)
+        modulate(0)
+        quantise_w(1, 1, w2_rounded, "wc11")
+        quantise_w(1, 0, w2_rounded, "feat0")
+        hb = [product(1, c) for c in range(NCH)]
+
+        g1 = keep.tile([P, 2, HALF], F32, name="g1", tag="w2_raw1", align_bytes=64)
         nc.scalar.activation(g1[:], g[2][:], COPY, bias=1.0)
-        v[2] = keep.tile([P, 2, HALF], F32, name="v2", align_bytes=64)
+        v[2] = keep.tile([P, 2, HALF], F32, name="v2", tag="wb10", align_bytes=64)
         nc.gpsimd.tensor_tensor(v[2][:], g1[:], feat_sb[2][:], MULT)
 
         yb0 = keep.tile([P, CH * PACK], BF16, name="yb0", align_bytes=64)
-        modulate(0)
         modulate(1)
         shift(0)
         shift(1)

@@ -25,7 +25,7 @@ NCH = S // CH
 
 
 def chunk(c):
-    return c // 2, 1 - c % 2
+    return divmod(c, 2)
 
 
 def tile_picked_zfilm_silu_po_kernel(tc, x_words, x_scales, w1, w2, feat, offs, out_0, out_1, out_2):
@@ -59,7 +59,12 @@ def tile_picked_zfilm_silu_po_kernel(tc, x_words, x_scales, w1, w2, feat, offs, 
         for c in range(NCH):
             h, u = chunk(c)
             f = keep.tile([P, 2, HALF], F32, name="feat%d" % c, tag="feat%d" % c, align_bytes=64)
-            nc.sync.dma_start(f[:], feat_rows[:, 2 * u : 2 * u + 2, h * HALF : (h + 1) * HALF])
+            rows = feat_rows[:, 2 * u : 2 * u + 2, h * HALF : (h + 1) * HALF]
+            if c == 0:
+                for e in range(2):
+                    nc.sync.dma_start(f[:, e, :], rows[:, e, :])
+            else:
+                nc.sync.dma_start(f[:], rows)
             feat_sb.append(f)
 
         warm = keep.tile([P, 1], F32, name="warm")
@@ -143,14 +148,15 @@ def tile_picked_zfilm_silu_po_kernel(tc, x_words, x_scales, w1, w2, feat, offs, 
             nc.scalar.activation(y[h][:, rows, :], u_sb[h][:, rows, :], SILU)
             nc.sync.dma_start(out_rows[:, rows, h * HALF : (h + 1) * HALF], y[h][:, rows, :])
 
-        modulate(0)
-        quantise_w(1, 1, w2_rounded, "wc11")
-        quantise_w(1, 0, w2_rounded, "feat0")
+        v[0] = keep.tile([P, 2, HALF], F32, name="v0", tag="v0", align_bytes=64)
+        for e in range(2):
+            nc.vector.scalar_tensor_tensor(v[0][:, e, :], g[0][:, e, :], 1.0, feat_sb[0][:, e, :], ADD, MULT)
+            quantise_w(1, e, w2_rounded, "wc1%d" % e)
         hb = [product(1, c) for c in range(NCH)]
 
         g1 = keep.tile([P, 2, HALF], F32, name="g1", tag="w2_raw1", align_bytes=64)
         nc.scalar.activation(g1[:], g[2][:], COPY, bias=1.0)
-        v[2] = keep.tile([P, 2, HALF], F32, name="v2", tag="wb10", align_bytes=64)
+        v[2] = keep.tile([P, 2, HALF], F32, name="v2", tag="wb11", align_bytes=64)
         nc.gpsimd.tensor_tensor(v[2][:], g1[:], feat_sb[2][:], MULT)
 
         yb0 = keep.tile([P, CH * PACK], BF16, name="yb0", align_bytes=64)

@@ -154,21 +154,23 @@ def tile_picked_zfilm_silu_po_kernel(tc, x_words, x_scales, w1, w2, feat, offs, 
             quantise_w(1, e, w2_rounded, "wc1%d" % e)
         hb = [product(1, c) for c in range(NCH)]
 
-        g1 = keep.tile([P, 2, HALF], F32, name="g1", tag="w2_raw1", align_bytes=64)
-        nc.scalar.activation(g1[:], g[2][:], COPY, bias=1.0)
+        g1 = keep.tile([P, 3, HALF], F32, name="g1", tag="w2_raw1", align_bytes=64)
+        nc.scalar.activation(g1[:, 0:2, :], g[2][:], COPY, bias=1.0)
+        nc.scalar.activation(g1[:, 2, :], g[3][:, 0, :], COPY, bias=1.0)
         v[2] = keep.tile([P, 2, HALF], F32, name="v2", tag="wb11", align_bytes=64)
-        nc.gpsimd.tensor_tensor(v[2][:], g1[:], feat_sb[2][:], MULT)
+        nc.gpsimd.tensor_tensor(v[2][:], g1[:, 0:2, :], feat_sb[2][:], MULT)
+        v[3] = keep.tile([P, 2, HALF], F32, name="v3", tag="v3", align_bytes=64)
+        nc.gpsimd.tensor_tensor(v[3][:, 0, :], g1[:, 2, :], feat_sb[3][:, 0, :], MULT)
 
-        yb0 = keep.tile([P, CH * PACK], BF16, name="yb0", align_bytes=64)
         modulate(1)
         shift(0)
         shift(1)
-        nc.scalar.activation(interleaved(yb0[:]), by_fours(u_sb[0], 0), SILU)
-        modulate(3)
+        nc.vector.scalar_tensor_tensor(v[3][:, 1, :], g[3][:, 1, :], 1.0, feat_sb[3][:, 1, :], ADD, MULT)
         shift(2)
         shift(3)
 
-        yb1 = keep.tile([P, CH * PACK], BF16, name="yb1", tag="v0", align_bytes=64)
+        yb0 = keep.tile([P, CH * PACK], BF16, name="yb0", tag="wb11", align_bytes=64)
+        yb1 = keep.tile([P, CH * PACK], BF16, name="yb1", tag="v3", align_bytes=64)
         yb2 = keep.tile([P, CH * PACK], BF16, name="yb2", align_bytes=64)
         yb3 = keep.tile([P, CH * PACK], BF16, name="yb3", align_bytes=64)
         y_codes = keep.tile([P, S], U32, name="y_codes", align_bytes=64)
@@ -181,11 +183,12 @@ def tile_picked_zfilm_silu_po_kernel(tc, x_words, x_scales, w1, w2, feat, offs, 
         def store_words(a, b):
             nc.sync.dma_start(out_words[:, PACK * a : PACK * b].bitcast(I32), y_codes[:, a:b].bitcast(I32))
 
-        quantise_y(0, yb0)
+        nc.vector.tensor_copy(interleaved(yb0[:]), by_fours(y[0], 0))
         nc.vector.tensor_copy(interleaved(yb1[:]), by_fours(y[0], 1))
-        nc.vector.tensor_copy(interleaved(yb2[:]), by_fours(y[1], 0))
+        quantise_y(0, yb0)
         quantise_y(1, yb1)
         store_words(0, HALF)
+        nc.vector.tensor_copy(interleaved(yb2[:]), by_fours(y[1], 0))
         quantise_y(2, yb2)
         quantise_y(3, yb3)
         store_words(HALF, S)

@@ -166,15 +166,24 @@ def tile_picked_zfilm_silu_po_kernel(tc, x_words, x_scales, w1, w2, feat, offs, 
         shift(0)
         shift(1)
         nc.vector.scalar_tensor_tensor(v[3][:, 1, :], g[3][:, 1, :], 1.0, feat_sb[3][:, 1, :], ADD, MULT)
-        shift(2)
-        shift(3)
+        for e in range(2):
+            nc.vector.tensor_tensor(u_sb[1][:, e, :], hb[2][:, e, :], v[2][:, e, :], ADD)
+            nc.scalar.activation(y[1][:, e, :], u_sb[1][:, e, :], SILU)
+        nc.sync.dma_start(out_rows[:, 0:2, HALF:S], y[1][:, 0:2, :])
+
+        yb3 = keep.tile([P, CH * PACK], BF16, name="yb3", align_bytes=64)
+        for k in range(2):
+            cols = slice(k * CH, (k + 1) * CH)
+            nc.vector.tensor_tensor(u_sb[1][:, 2:4, cols], hb[3][:, :, cols], v[3][:, :, cols], ADD)
+        nc.scalar.activation(y[1][:, 2:4, 0:CH], u_sb[1][:, 2:4, 0:CH], SILU)
+        nc.scalar.activation(y[1][:, 2:4, CH:HALF], u_sb[1][:, 2:4, CH:HALF], SILU)
+        nc.scalar.activation(interleaved(yb3[:]), by_fours(u_sb[1], 1), SILU)
+        nc.sync.dma_start(out_rows[:, 2:4, HALF:S], y[1][:, 2:4, :])
 
         yb0 = keep.tile([P, CH * PACK], BF16, name="yb0", tag="wb11", align_bytes=64)
         yb1 = keep.tile([P, CH * PACK], BF16, name="yb1", tag="v3", align_bytes=64)
         yb2 = keep.tile([P, CH * PACK], BF16, name="yb2", align_bytes=64)
-        yb3 = keep.tile([P, CH * PACK], BF16, name="yb3", align_bytes=64)
         y_codes = keep.tile([P, S], U32, name="y_codes", align_bytes=64)
-        nc.scalar.activation(interleaved(yb3[:]), by_fours(u_sb[1], 1), SILU)
 
         def quantise_y(c, src):
             cols = slice(c * CH, (c + 1) * CH)
@@ -189,8 +198,8 @@ def tile_picked_zfilm_silu_po_kernel(tc, x_words, x_scales, w1, w2, feat, offs, 
         quantise_y(1, yb1)
         store_words(0, HALF)
         nc.vector.tensor_copy(interleaved(yb2[:]), by_fours(y[1], 0))
-        quantise_y(2, yb2)
         quantise_y(3, yb3)
+        quantise_y(2, yb2)
         store_words(HALF, S)
         for q in range(4):
             eng = nc.scalar if q % 2 == 0 else nc.sync

@@ -2,7 +2,7 @@ from contextlib import ExitStack
 
 import concourse.mybir as mybir
 
-K, T, S, N = 512, 2048, 512, 512
+T, S, N, K = 2048, 512, 512, 512
 FLOPS = 2 * 2 * K * N * S
 
 F32 = mybir.dt.float32
@@ -20,12 +20,10 @@ SILU = mybir.ActivationFunctionType.Silu
 P = 128
 PACK = 4
 HALF = S // 2
-CH = 128
-NCH = S // CH
-
-
-def chunk(c):
-    return divmod(c, 2)
+QUARTER = S // 4
+CHUNKS = 4
+PER_COLUMN = 16
+RUN = 4
 
 
 def tile_picked_zfilm_silu_po_kernel(tc, x_words, x_scales, w1, w2, feat, offs, out_0, out_1, out_2):
@@ -34,13 +32,9 @@ def tile_picked_zfilm_silu_po_kernel(tc, x_words, x_scales, w1, w2, feat, offs, 
         keep = ctx.enter_context(tc.tile_pool(name="keep", bufs=1))
         psum = ctx.enter_context(tc.psum_pool(name="psum", bufs=1))
 
-        def load_columns(src, a, b, name):
-            tile = keep.tile([P, PACK, b - a], F32, name=name, tag=name, align_bytes=64)
-            nc.sync.dma_start(tile[:], src.rearrange("(p j) c -> p j c", j=PACK)[:, :, a:b])
-            return tile
-
-        w1_raw = load_columns(w1, 0, N, "w1_raw")
-        offsets = keep.tile([P, S // 16], U16, name="offsets")
+        w1_raw = keep.tile([P, PACK, N], F32, name="w1_raw", tag="w1_raw", align_bytes=64)
+        nc.sync.dma_start(w1_raw[:], w1.rearrange("(p j) c -> p j c", j=PACK)[:, :, 0:N])
+        offsets = keep.tile([P, S // PER_COLUMN], U16, name="offsets")
         nc.sync.dma_start(offsets[:], offs)
         table_scales = keep.tile([P, T], U8, name="table_scales", align_bytes=64)
         nc.vector.memset(table_scales[:].bitcast(I32), 0)
@@ -50,14 +44,14 @@ def tile_picked_zfilm_silu_po_kernel(tc, x_words, x_scales, w1, w2, feat, offs, 
         nc.sync.dma_start(table_words[:].bitcast(I32), x_words[0].rearrange("p n t -> p (n t)").bitcast(I32))
         w2_rows = w2.rearrange("(p j) c -> p j c", j=PACK)
         w2_raw = []
-        for k in range(2):
-            raw = keep.tile([P, 2, N], F32, name="w2_raw%d" % k, tag="w2_raw%d" % k, align_bytes=64)
-            nc.sync.dma_start(raw[:], w2_rows[:, 2 * k : 2 * k + 2, :])
+        for pair in range(2):
+            raw = keep.tile([P, 2, N], F32, name="w2_raw%d" % pair, tag="w2_raw%d" % pair, align_bytes=64)
+            nc.sync.dma_start(raw[:], w2_rows[:, 2 * pair : 2 * pair + 2, :])
             w2_raw.append(raw)
         feat_rows = feat.rearrange("(p t) s -> p t s", t=PACK)
         feat_sb = []
-        for c in range(NCH):
-            h, u = chunk(c)
+        for c in range(CHUNKS):
+            h, u = divmod(c, 2)
             f = keep.tile([P, 2, HALF], F32, name="feat%d" % c, tag="feat%d" % c, align_bytes=64)
             rows = feat_rows[:, 2 * u : 2 * u + 2, h * HALF : (h + 1) * HALF]
             if c == 0:
@@ -70,24 +64,24 @@ def tile_picked_zfilm_silu_po_kernel(tc, x_words, x_scales, w1, w2, feat, offs, 
         warm = keep.tile([P, 1], F32, name="warm")
         nc.scalar.activation(warm[:], w1_raw[:, 0, 0:1], SILU)
 
-        x_sc = keep.tile([P, S], U8, name="x_sc", align_bytes=64)
-        nc.vector.tensor_copy(x_sc[:], table_scales[:].indirect(offsets[:]))
+        picked_scales = keep.tile([P, S], U8, name="picked_scales", align_bytes=64)
+        nc.vector.tensor_copy(picked_scales[:], table_scales[:].indirect(offsets[:]))
 
         w_codes = {}
         w_scales = {}
 
-        def round_w(i, raws):
+        def round_weight(i, raws):
             rounded = [keep.tile([P, 2, P * PACK], BF16, name="wb%d%d" % (i, u), tag="wb%d%d" % (i, u), align_bytes=64) for u in range(2)]
-            rows = PACK // len(raws)
-            for k, raw in enumerate(raws):
+            rows_per_load = PACK // len(raws)
+            for n, raw in enumerate(raws):
                 dealt = raw[:].rearrange("p j (m t) -> p m j t", t=PACK)
-                dst = [r[:].rearrange("p t (m j) -> p m j t", j=PACK)[:, :, k * rows : (k + 1) * rows, :] for r in rounded]
+                dst = [r[:].rearrange("p t (m j) -> p m j t", j=PACK)[:, :, n * rows_per_load : (n + 1) * rows_per_load, :] for r in rounded]
                 nc.vector.tensor_copy(dst[0], dealt[:, :, :, 0:2])
                 nc.scalar.copy(dst[1], dealt[:, :, :, 2:4])
             return rounded
 
-        def quantise_w(i, u, rounded, tag):
-            w_codes[i, u] = keep.tile([P, 2, P], U32, name="wc%d%d" % (i, u), tag=tag, align_bytes=64)
+        def quantise_weight(i, u, rounded):
+            w_codes[i, u] = keep.tile([P, 2, P], U32, name="wc%d%d" % (i, u), tag="wc%d%d" % (i, u), align_bytes=64)
             w_scales[i, u] = keep.tile([P, 2, P], U8, name="ws%d%d" % (i, u), align_bytes=64)
             nc.vector.quantize_mx(
                 out=w_codes[i, u][:].rearrange("p e m -> p (e m)").bitcast(FP8X4),
@@ -95,112 +89,110 @@ def tile_picked_zfilm_silu_po_kernel(tc, x_words, x_scales, w1, w2, feat, offs, 
                 in_=rounded[u][:].rearrange("p e c -> p (e c)"),
             )
 
-        w1_rounded = round_w(0, [w1_raw])
+        w1_rounded = round_weight(0, [w1_raw])
         for u in range(2):
-            quantise_w(0, u, w1_rounded, "wc0%d" % u)
+            quantise_weight(0, u, w1_rounded)
 
-        x_codes = []
+        picked_words = []
         for h in range(2):
-            xc = keep.tile([P, HALF], U32, name="x_codes%d" % h, align_bytes=64)
-            nc.vector.tensor_copy(xc[:], table_words[:].indirect(offsets[:, h * (HALF // 16) : (h + 1) * (HALF // 16)]))
-            x_codes.append(xc)
+            words = keep.tile([P, HALF], U32, name="picked_words%d" % h, align_bytes=64)
+            nc.vector.tensor_copy(words[:], table_words[:].indirect(offsets[:, h * (HALF // PER_COLUMN) : (h + 1) * (HALF // PER_COLUMN)]))
+            picked_words.append(words)
 
         def product(i, c):
             bank = psum.tile([P, 2, HALF], F32, name="bank%d%d" % (i, c))
-            h, u = chunk(c)
+            h, u = divmod(c, 2)
             for e in range(2):
                 nc.tensor.matmul_mx(
                     out=bank[:, e, :],
                     lhsT=w_codes[i, u][:, e, :].bitcast(FP8X4),
                     lhsT_scale=w_scales[i, u][:, e, :],
-                    rhs=x_codes[h][:].bitcast(FP8X4),
-                    rhs_scale=x_sc[:, h * HALF : (h + 1) * HALF],
+                    rhs=picked_words[h][:].bitcast(FP8X4),
+                    rhs_scale=picked_scales[:, h * HALF : (h + 1) * HALF],
                     start=True,
                     stop=True,
                 )
             return bank
 
-        g = [product(0, c) for c in range(NCH)]
-        w2_rounded = round_w(1, w2_raw)
+        g_banks = [product(0, c) for c in range(CHUNKS)]
+        w2_rounded = round_weight(1, w2_raw)
 
         y_scales = keep.tile([P, S], U8, name="y_scales", align_bytes=64)
         out_rows = out_0.rearrange("(p t) s -> p t s", t=PACK)
         out_words = out_1[0].rearrange("p n t -> p (n t)")
 
-        v = {}
-        u_sb = [keep.tile([P, PACK, HALF], F32, name="u%d" % h, align_bytes=64) for h in range(2)]
+        scaled = {}
+        summed = [keep.tile([P, PACK, HALF], F32, name="summed%d" % h, align_bytes=64) for h in range(2)]
         y = [keep.tile([P, PACK, HALF], F32, name="y%d" % h, align_bytes=64) for h in range(2)]
 
         def interleaved(ap):
-            return ap.rearrange("p (a i t) -> p a t i", i=4, t=PACK)
+            return ap.rearrange("p (a i t) -> p a t i", i=RUN, t=PACK)
 
-        def by_fours(tile, k):
-            return tile[:, :, k * CH : (k + 1) * CH].rearrange("p t (a i) -> p a t i", i=4)
+        def by_runs(tile, k):
+            return tile[:, :, k * QUARTER : (k + 1) * QUARTER].rearrange("p t (a i) -> p a t i", i=RUN)
 
-        def modulate(c):
-            v[c] = keep.tile([P, 2, HALF], F32, name="v%d" % c, tag="v%d" % (c % 3), align_bytes=64)
-            nc.vector.scalar_tensor_tensor(v[c][:], g[c][:], 1.0, feat_sb[c][:], ADD, MULT)
-
-        def shift(c):
-            h, u = chunk(c)
+        def finish_chunk(c):
+            h, u = divmod(c, 2)
             rows = slice(2 * u, 2 * u + 2)
-            nc.vector.tensor_tensor(u_sb[h][:, rows, :], hb[c][:], v[c][:], ADD)
-            nc.scalar.activation(y[h][:, rows, :], u_sb[h][:, rows, :], SILU)
+            nc.vector.tensor_tensor(summed[h][:, rows, :], h_banks[c][:], scaled[c][:], ADD)
+            nc.scalar.activation(y[h][:, rows, :], summed[h][:, rows, :], SILU)
             nc.sync.dma_start(out_rows[:, rows, h * HALF : (h + 1) * HALF], y[h][:, rows, :])
 
-        v[0] = keep.tile([P, 2, HALF], F32, name="v0", tag="v0", align_bytes=64)
+        scaled[0] = keep.tile([P, 2, HALF], F32, name="scaled0", tag="scaled0", align_bytes=64)
         for e in range(2):
-            nc.vector.scalar_tensor_tensor(v[0][:, e, :], g[0][:, e, :], 1.0, feat_sb[0][:, e, :], ADD, MULT)
-            quantise_w(1, e, w2_rounded, "wc1%d" % e)
-        hb = [product(1, c) for c in range(NCH)]
+            nc.vector.scalar_tensor_tensor(scaled[0][:, e, :], g_banks[0][:, e, :], 1.0, feat_sb[0][:, e, :], ADD, MULT)
+            quantise_weight(1, e, w2_rounded)
+        h_banks = [product(1, c) for c in range(CHUNKS)]
 
-        g1 = keep.tile([P, 3, HALF], F32, name="g1", tag="w2_raw1", align_bytes=64)
-        nc.scalar.activation(g1[:, 0:2, :], g[2][:], COPY, bias=1.0)
-        nc.scalar.activation(g1[:, 2, :], g[3][:, 0, :], COPY, bias=1.0)
-        v[2] = keep.tile([P, 2, HALF], F32, name="v2", tag="wb11", align_bytes=64)
-        nc.gpsimd.tensor_tensor(v[2][:], g1[:, 0:2, :], feat_sb[2][:], MULT)
-        v[3] = keep.tile([P, 2, HALF], F32, name="v3", tag="v3", align_bytes=64)
-        nc.gpsimd.tensor_tensor(v[3][:, 0, :], g1[:, 2, :], feat_sb[3][:, 0, :], MULT)
+        g_plus_1 = keep.tile([P, 3, HALF], F32, name="g_plus_1", tag="w2_raw1", align_bytes=64)
+        nc.scalar.activation(g_plus_1[:, 0, :], g_banks[2][:, 1, :], COPY, bias=1.0)
+        nc.scalar.activation(g_plus_1[:, 1:3, :], g_banks[3][:], COPY, bias=1.0)
+        scaled_slice1 = keep.tile([P, HALF], F32, name="scaled_slice1", tag="wb11", align_bytes=64)
+        nc.gpsimd.tensor_tensor(scaled_slice1[:], g_plus_1[:, 0, :], feat_sb[2][:, 1, :], MULT)
+        scaled[3] = keep.tile([P, 2, HALF], F32, name="scaled3", tag="scaled3", align_bytes=64)
+        nc.gpsimd.tensor_tensor(scaled[3][:], g_plus_1[:, 1:3, :], feat_sb[3][:], MULT)
 
-        modulate(1)
-        shift(0)
-        shift(1)
-        nc.vector.scalar_tensor_tensor(v[3][:, 1, :], g[3][:, 1, :], 1.0, feat_sb[3][:, 1, :], ADD, MULT)
-        for e in range(2):
-            nc.vector.tensor_tensor(u_sb[1][:, e, :], hb[2][:, e, :], v[2][:, e, :], ADD)
-            nc.scalar.activation(y[1][:, e, :], u_sb[1][:, e, :], SILU)
+        scaled[1] = keep.tile([P, 2, HALF], F32, name="scaled1", tag="scaled1", align_bytes=64)
+        nc.vector.scalar_tensor_tensor(scaled[1][:], g_banks[1][:], 1.0, feat_sb[1][:], ADD, MULT)
+        finish_chunk(0)
+        finish_chunk(1)
+        scaled_slice0 = keep.tile([P, HALF], F32, name="scaled_slice0", tag="scaled0", align_bytes=64)
+        nc.vector.scalar_tensor_tensor(scaled_slice0[:], g_banks[2][:, 0, :], 1.0, feat_sb[2][:, 0, :], ADD, MULT)
+        for e, src in ((1, scaled_slice1), (0, scaled_slice0)):
+            nc.vector.tensor_tensor(summed[1][:, e, :], h_banks[2][:, e, :], src[:], ADD)
+            nc.scalar.activation(y[1][:, e, :], summed[1][:, e, :], SILU)
         nc.sync.dma_start(out_rows[:, 0:2, HALF:S], y[1][:, 0:2, :])
 
-        yb3 = keep.tile([P, CH * PACK], BF16, name="yb3", align_bytes=64)
+        yb3 = keep.tile([P, QUARTER * PACK], BF16, name="yb3", align_bytes=64)
         for k in range(2):
-            cols = slice(k * CH, (k + 1) * CH)
-            nc.vector.tensor_tensor(u_sb[1][:, 2:4, cols], hb[3][:, :, cols], v[3][:, :, cols], ADD)
-        nc.scalar.activation(y[1][:, 2:4, 0:CH], u_sb[1][:, 2:4, 0:CH], SILU)
-        nc.scalar.activation(y[1][:, 2:4, CH:HALF], u_sb[1][:, 2:4, CH:HALF], SILU)
-        nc.scalar.activation(interleaved(yb3[:]), by_fours(u_sb[1], 1), SILU)
+            cols = slice(k * QUARTER, (k + 1) * QUARTER)
+            nc.vector.tensor_tensor(summed[1][:, 2:4, cols], h_banks[3][:, :, cols], scaled[3][:, :, cols], ADD)
+        nc.scalar.activation(y[1][:, 2:4, 0:QUARTER], summed[1][:, 2:4, 0:QUARTER], SILU)
+        nc.scalar.activation(y[1][:, 2:4, QUARTER:HALF], summed[1][:, 2:4, QUARTER:HALF], SILU)
+        nc.scalar.activation(interleaved(yb3[:]), by_runs(summed[1], 1), SILU)
         nc.sync.dma_start(out_rows[:, 2:4, HALF:S], y[1][:, 2:4, :])
 
-        yb0 = keep.tile([P, CH * PACK], BF16, name="yb0", tag="wb11", align_bytes=64)
-        yb1 = keep.tile([P, CH * PACK], BF16, name="yb1", tag="v3", align_bytes=64)
-        yb2 = keep.tile([P, CH * PACK], BF16, name="yb2", align_bytes=64)
+        yb0 = keep.tile([P, QUARTER * PACK], BF16, name="yb0", tag="wb11", align_bytes=64)
+        yb1 = keep.tile([P, QUARTER * PACK], BF16, name="yb1", tag="scaled3", align_bytes=64)
+        yb2 = keep.tile([P, QUARTER * PACK], BF16, name="yb2", align_bytes=64)
         y_codes = keep.tile([P, S], U32, name="y_codes", align_bytes=64)
 
-        def quantise_y(c, src):
-            cols = slice(c * CH, (c + 1) * CH)
+        def quantise_y(quarter, src):
+            cols = slice(quarter * QUARTER, (quarter + 1) * QUARTER)
             nc.vector.quantize_mx(out=y_codes[:, cols].bitcast(FP8X4), scales=y_scales[:, cols], in_=src[:])
 
         def store_words(a, b):
             nc.sync.dma_start(out_words[:, PACK * a : PACK * b].bitcast(I32), y_codes[:, a:b].bitcast(I32))
 
-        nc.vector.tensor_copy(interleaved(yb0[:]), by_fours(y[0], 0))
-        nc.vector.tensor_copy(interleaved(yb1[:]), by_fours(y[0], 1))
+        nc.vector.tensor_copy(interleaved(yb0[:]), by_runs(y[0], 0))
+        nc.vector.tensor_copy(interleaved(yb1[:]), by_runs(y[0], 1))
         quantise_y(0, yb0)
         quantise_y(1, yb1)
         store_words(0, HALF)
-        nc.vector.tensor_copy(interleaved(yb2[:]), by_fours(y[1], 0))
+        nc.vector.tensor_copy(interleaved(yb2[:]), by_runs(y[1], 0))
         quantise_y(3, yb3)
         quantise_y(2, yb2)
         store_words(HALF, S)
         for q in range(4):
-            eng = nc.scalar if q % 2 == 0 else nc.sync
-            eng.dma_start(out_2[0, 4 * q : 4 * q + 4, :].bitcast(I32), y_scales[32 * q : 32 * q + 4, :].bitcast(I32))
+            queue = nc.scalar if q % 2 == 0 else nc.sync
+            queue.dma_start(out_2[0, 4 * q : 4 * q + 4, :].bitcast(I32), y_scales[32 * q : 32 * q + 4, :].bitcast(I32))

@@ -23,7 +23,7 @@ HALF = S // 2
 QUARTER = S // 4
 CHUNKS = 4
 PER_COLUMN = 16
-RUN = 4
+RUN = 2
 
 
 def tile_picked_zfilm_silu_po_kernel(tc, x_words, x_scales, w1, w2, feat, offs, out_0, out_1, out_2):
@@ -73,11 +73,13 @@ def tile_picked_zfilm_silu_po_kernel(tc, x_words, x_scales, w1, w2, feat, offs, 
         def round_weight(i, raws):
             rounded = [keep.tile([P, 2, P * PACK], BF16, name="wb%d%d" % (i, u), tag="wb%d%d" % (i, u), align_bytes=64) for u in range(2)]
             rows_per_load = PACK // len(raws)
+            walk = "p m j t" if rows_per_load == PACK else "p m t j"
             for n, raw in enumerate(raws):
-                dealt = raw[:].rearrange("p j (m t) -> p m j t", t=PACK)
-                dst = [r[:].rearrange("p t (m j) -> p m j t", j=PACK)[:, :, n * rows_per_load : (n + 1) * rows_per_load, :] for r in rounded]
-                nc.vector.tensor_copy(dst[0], dealt[:, :, :, 0:2])
-                nc.scalar.copy(dst[1], dealt[:, :, :, 2:4])
+                rows = slice(n * rows_per_load, (n + 1) * rows_per_load)
+                dealt = raw[:].rearrange("p j (m t) -> p j m t", t=PACK)
+                for u, copy in enumerate((nc.vector.tensor_copy, nc.scalar.copy)):
+                    dst = rounded[u][:].rearrange("p t (m j) -> p j m t", j=PACK)[:, rows]
+                    copy(dst.rearrange("p j m t -> " + walk), dealt[:, :, :, 2 * u : 2 * u + 2].rearrange("p j m t -> " + walk))
             return rounded
 
         def quantise_weight(i, u, rounded):

@@ -23,6 +23,7 @@ HALF = S // 2
 QUARTER = S // 4
 CHUNKS = 4
 PER_COLUMN = 16
+SHARE = 40
 RUN = 2
 
 
@@ -33,13 +34,15 @@ def tile_picked_zfilm_silu_po_kernel(tc, x_words, x_scales, w1, w2, feat, offs, 
         psum = ctx.enter_context(tc.psum_pool(name="psum", bufs=1))
 
         w1_raw = keep.tile([P, PACK, N], F32, name="w1_raw", tag="w1_raw", align_bytes=64)
-        nc.sync.dma_start(w1_raw[:], w1.rearrange("(p j) c -> p j c", j=PACK)[:, :, 0:N])
+        w1_rows = w1.rearrange("(p j) c -> p j c", j=PACK)
+        nc.sync.dma_start(w1_raw[:, 0:2, :], w1_rows[:, 0:2, :])
         offsets = keep.tile([P, S // PER_COLUMN], U16, name="offsets")
         nc.sync.dma_start(offsets[:], offs)
         table_scales = keep.tile([P, T], U8, name="table_scales", align_bytes=64)
         nc.vector.memset(table_scales[:].bitcast(I32), 0)
         for q in range(4):
             nc.sync.dma_start(table_scales[32 * q : 32 * q + 4, :].bitcast(I32), x_scales[0, 4 * q : 4 * q + 4, :].bitcast(I32))
+        nc.sync.dma_start(w1_raw[:, 2:4, :], w1_rows[:, 2:4, :])
         table_words = keep.tile([P, T], U32, name="table_words", align_bytes=64)
         nc.sync.dma_start(table_words[:].bitcast(I32), x_words[0].rearrange("p n t -> p (n t)").bitcast(I32))
         w2_rows = w2.rearrange("(p j) c -> p j c", j=PACK)
@@ -49,20 +52,16 @@ def tile_picked_zfilm_silu_po_kernel(tc, x_words, x_scales, w1, w2, feat, offs, 
             nc.sync.dma_start(raw[:], w2_rows[:, 2 * pair : 2 * pair + 2, :])
             w2_raw.append(raw)
         feat_rows = feat.rearrange("(p t) s -> p t s", t=PACK)
-        feat_sb = []
-        for c in range(CHUNKS):
-            h, u = divmod(c, 2)
-            f = keep.tile([P, 2, HALF], F32, name="feat%d" % c, tag="feat%d" % c, align_bytes=64)
-            rows = feat_rows[:, 2 * u : 2 * u + 2, h * HALF : (h + 1) * HALF]
-            if c == 0:
-                for e in range(2):
-                    nc.sync.dma_start(f[:, e, :], rows[:, e, :])
-            else:
-                nc.sync.dma_start(f[:], rows)
-            feat_sb.append(f)
+        feat_sb = {}
+        for h, first, last in ((0, 0, 2), (0, 2, 4), (1, 0, 2), (1, 2, 4)):
+            f = keep.tile([P, last - first, HALF], F32, name="feat%d%d" % (h, first), align_bytes=64)
+            nc.sync.dma_start(f[:], feat_rows[:, first:last, h * HALF : (h + 1) * HALF])
+            feat_sb[h, first] = f
 
+        zero = keep.tile([P, 1], F32, name="zero")
+        nc.gpsimd.memset(zero[:], 0.0)
         warm = keep.tile([P, 1], F32, name="warm")
-        nc.scalar.activation(warm[:], w1_raw[:, 0, 0:1], SILU)
+        nc.scalar.activation(warm[:], zero[:], SILU)
 
         picked_scales = keep.tile([P, S], U8, name="picked_scales", align_bytes=64)
         nc.vector.tensor_copy(picked_scales[:], table_scales[:].indirect(offsets[:]))
@@ -70,35 +69,41 @@ def tile_picked_zfilm_silu_po_kernel(tc, x_words, x_scales, w1, w2, feat, offs, 
         w_codes = {}
         w_scales = {}
 
-        def round_weight(i, raws):
-            rounded = [keep.tile([P, 2, P * PACK], BF16, name="wb%d%d" % (i, u), tag="wb%d%d" % (i, u), align_bytes=64) for u in range(2)]
-            rows_per_load = PACK // len(raws)
-            walk = "p m j t" if rows_per_load == PACK else "p m t j"
-            for n, raw in enumerate(raws):
-                rows = slice(n * rows_per_load, (n + 1) * rows_per_load)
-                dealt = raw[:].rearrange("p j (m t) -> p j m t", t=PACK)
-                for u, copy in enumerate((nc.vector.tensor_copy, nc.scalar.copy)):
-                    dst = rounded[u][:].rearrange("p t (m j) -> p j m t", j=PACK)[:, rows]
-                    copy(dst.rearrange("p j m t -> " + walk), dealt[:, :, :, 2 * u : 2 * u + 2].rearrange("p j m t -> " + walk))
-            return rounded
+        rounded = {
+            (i, u): keep.tile([P, 2, P * PACK], BF16, name="wb%d%d" % (i, u), tag="wb%d%d" % (i, u), align_bytes=64)
+            for i in range(2)
+            for u in range(2)
+        }
+        for key in rounded:
+            w_codes[key] = keep.tile([P, 2, P], U32, name="wc%d%d" % key, align_bytes=64)
+            w_scales[key] = keep.tile([P, 2, P], U8, name="ws%d%d" % key, align_bytes=64)
 
-        def quantise_weight(i, u, rounded):
-            w_codes[i, u] = keep.tile([P, 2, P], U32, name="wc%d%d" % (i, u), tag="wc%d%d" % (i, u), align_bytes=64)
-            w_scales[i, u] = keep.tile([P, 2, P], U8, name="ws%d%d" % (i, u), align_bytes=64)
+        def round_weight(copy, i, raw, rows, slices, ms=slice(0, P)):
+            u, first = divmod(slices.start, 2)
+            walk = "p j m t -> p m j t" if rows.stop - rows.start == PACK else "p j m t -> p m t j"
+            dst = rounded[i, u][:].rearrange("p t (m j) -> p j m t", j=PACK)[:, rows, ms, first : first + slices.stop - slices.start]
+            copy(dst.rearrange(walk), raw[:].rearrange("p j (m t) -> p j m t", t=PACK)[:, :, ms, slices].rearrange(walk))
+
+        def quantise_weight(i, slices):
+            u, first = divmod(slices.start, 2)
+            part = slice(first, first + slices.stop - slices.start)
             nc.vector.quantize_mx(
-                out=w_codes[i, u][:].rearrange("p e m -> p (e m)").bitcast(FP8X4),
-                scales=w_scales[i, u][:].rearrange("p e m -> p (e m)"),
-                in_=rounded[u][:].rearrange("p e c -> p (e c)"),
+                out=w_codes[i, u][:, part, :].rearrange("p e m -> p (e m)").bitcast(FP8X4),
+                scales=w_scales[i, u][:, part, :].rearrange("p e m -> p (e m)"),
+                in_=rounded[i, u][:, part, :].rearrange("p e c -> p (e c)"),
             )
 
-        w1_rounded = round_weight(0, [w1_raw])
-        for u in range(2):
-            quantise_weight(0, u, w1_rounded)
+        pairs = (slice(0, 2), slice(2, 4))
+        round_weight(nc.vector.tensor_copy, 0, w1_raw, slice(0, PACK), pairs[0])
+        round_weight(nc.scalar.copy, 0, w1_raw, slice(0, PACK), pairs[1])
+        for pair in pairs:
+            quantise_weight(0, pair)
 
         picked_words = []
         for h in range(2):
+            entries = offsets[:, h * (HALF // PER_COLUMN) : (h + 1) * (HALF // PER_COLUMN)]
             words = keep.tile([P, HALF], U32, name="picked_words%d" % h, align_bytes=64)
-            nc.vector.tensor_copy(words[:], table_words[:].indirect(offsets[:, h * (HALF // PER_COLUMN) : (h + 1) * (HALF // PER_COLUMN)]))
+            nc.vector.tensor_copy(words[:], table_words[:].indirect(entries))
             picked_words.append(words)
 
         def product(i, c):
@@ -116,8 +121,14 @@ def tile_picked_zfilm_silu_po_kernel(tc, x_words, x_scales, w1, w2, feat, offs, 
                 )
             return bank
 
-        g_banks = [product(0, c) for c in range(CHUNKS)]
-        w2_rounded = round_weight(1, w2_raw)
+        g_banks = {c: product(0, c) for c in range(CHUNKS)}
+        round_weight(nc.vector.tensor_copy, 1, w2_raw[0], pairs[0], pairs[0])
+        round_weight(nc.scalar.copy, 1, w2_raw[0], pairs[0], pairs[1])
+        round_weight(nc.scalar.copy, 1, w2_raw[1], pairs[1], pairs[1], slice(SHARE, P))
+        round_weight(nc.vector.tensor_copy, 1, w2_raw[1], pairs[1], pairs[0])
+        round_weight(nc.vector.tensor_copy, 1, w2_raw[1], pairs[1], pairs[1], slice(0, SHARE))
+        for pair in pairs:
+            quantise_weight(1, pair)
 
         y_scales = keep.tile([P, S], U8, name="y_scales", align_bytes=64)
         out_rows = out_0.rearrange("(p t) s -> p t s", t=PACK)
@@ -141,25 +152,32 @@ def tile_picked_zfilm_silu_po_kernel(tc, x_words, x_scales, w1, w2, feat, offs, 
             nc.sync.dma_start(out_rows[:, rows, h * HALF : (h + 1) * HALF], y[h][:, rows, :])
 
         scaled[0] = keep.tile([P, 2, HALF], F32, name="scaled0", tag="scaled0", align_bytes=64)
-        for e in range(2):
-            nc.vector.scalar_tensor_tensor(scaled[0][:, e, :], g_banks[0][:, e, :], 1.0, feat_sb[0][:, e, :], ADD, MULT)
-            quantise_weight(1, e, w2_rounded)
+        nc.vector.scalar_tensor_tensor(scaled[0][:], g_banks[0][:], 1.0, feat_sb[0, 0][:], ADD, MULT)
         h_banks = [product(1, c) for c in range(CHUNKS)]
 
-        g_plus_1 = keep.tile([P, 3, HALF], F32, name="g_plus_1", tag="w2_raw1", align_bytes=64)
-        nc.scalar.activation(g_plus_1[:, 0, :], g_banks[2][:, 1, :], COPY, bias=1.0)
-        nc.scalar.activation(g_plus_1[:, 1:3, :], g_banks[3][:], COPY, bias=1.0)
-        scaled_slice1 = keep.tile([P, HALF], F32, name="scaled_slice1", tag="wb11", align_bytes=64)
-        nc.gpsimd.tensor_tensor(scaled_slice1[:], g_plus_1[:, 0, :], feat_sb[2][:, 1, :], MULT)
-        scaled[3] = keep.tile([P, 2, HALF], F32, name="scaled3", tag="scaled3", align_bytes=64)
-        nc.gpsimd.tensor_tensor(scaled[3][:], g_plus_1[:, 1:3, :], feat_sb[3][:], MULT)
-
-        scaled[1] = keep.tile([P, 2, HALF], F32, name="scaled1", tag="scaled1", align_bytes=64)
-        nc.vector.scalar_tensor_tensor(scaled[1][:], g_banks[1][:], 1.0, feat_sb[1][:], ADD, MULT)
+        g_plus_1 = keep.tile([P, 4, HALF], F32, name="g_plus_1", tag="w2_raw1", align_bytes=64)
+        nc.scalar.activation(g_plus_1[:, 0, :], g_banks[1][:, 1, :], COPY, bias=1.0)
+        nc.scalar.activation(g_plus_1[:, 1, :], g_banks[2][:, 1, :], COPY, bias=1.0)
+        nc.scalar.activation(g_plus_1[:, 2:4, :], g_banks[3][:], COPY, bias=1.0)
+        scaled_slice3 = keep.tile([P, HALF], F32, name="scaled_slice3", tag="wb11", align_bytes=64)
+        nc.gpsimd.tensor_tensor(scaled_slice3[:], g_plus_1[:, 0, :], feat_sb[0, 2][:, 1, :], MULT)
+        scaled_slice1 = keep.tile([P, HALF], F32, name="scaled_slice1", align_bytes=64)
+        nc.gpsimd.tensor_tensor(scaled_slice1[:], g_plus_1[:, 1, :], feat_sb[1, 0][:, 1, :], MULT)
+        scaled_last = []
+        for k in range(2):
+            cols = slice(k * QUARTER, (k + 1) * QUARTER)
+            part = keep.tile([P, 2, QUARTER], F32, name="scaled_last%d" % k, tag="scaled_last%d" % k, align_bytes=64)
+            nc.gpsimd.tensor_tensor(part[:], g_plus_1[:, 2:4, cols], feat_sb[1, 2][:, :, cols], MULT)
+            scaled_last.append(part)
+        scaled_slice2 = keep.tile([P, HALF], F32, name="scaled_slice2", align_bytes=64)
+        nc.vector.scalar_tensor_tensor(scaled_slice2[:], g_banks[1][:, 0, :], 1.0, feat_sb[0, 2][:, 0, :], ADD, MULT)
         finish_chunk(0)
-        finish_chunk(1)
+        for e, src in enumerate((scaled_slice2, scaled_slice3)):
+            nc.vector.tensor_tensor(summed[0][:, 2 + e, :], h_banks[1][:, e, :], src[:], ADD)
+        nc.scalar.activation(y[0][:, 2:4, :], summed[0][:, 2:4, :], SILU)
+        nc.sync.dma_start(out_rows[:, 2:4, 0:HALF], y[0][:, 2:4, :])
         scaled_slice0 = keep.tile([P, HALF], F32, name="scaled_slice0", tag="scaled0", align_bytes=64)
-        nc.vector.scalar_tensor_tensor(scaled_slice0[:], g_banks[2][:, 0, :], 1.0, feat_sb[2][:, 0, :], ADD, MULT)
+        nc.vector.scalar_tensor_tensor(scaled_slice0[:], g_banks[2][:, 0, :], 1.0, feat_sb[1, 0][:, 0, :], ADD, MULT)
         for e, src in ((1, scaled_slice1), (0, scaled_slice0)):
             nc.vector.tensor_tensor(summed[1][:, e, :], h_banks[2][:, e, :], src[:], ADD)
             nc.scalar.activation(y[1][:, e, :], summed[1][:, e, :], SILU)
@@ -168,14 +186,14 @@ def tile_picked_zfilm_silu_po_kernel(tc, x_words, x_scales, w1, w2, feat, offs, 
         yb3 = keep.tile([P, QUARTER * PACK], BF16, name="yb3", align_bytes=64)
         for k in range(2):
             cols = slice(k * QUARTER, (k + 1) * QUARTER)
-            nc.vector.tensor_tensor(summed[1][:, 2:4, cols], h_banks[3][:, :, cols], scaled[3][:, :, cols], ADD)
+            nc.vector.tensor_tensor(summed[1][:, 2:4, cols], h_banks[3][:, :, cols], scaled_last[k][:], ADD)
         nc.scalar.activation(y[1][:, 2:4, 0:QUARTER], summed[1][:, 2:4, 0:QUARTER], SILU)
         nc.scalar.activation(y[1][:, 2:4, QUARTER:HALF], summed[1][:, 2:4, QUARTER:HALF], SILU)
         nc.scalar.activation(interleaved(yb3[:]), by_runs(summed[1], 1), SILU)
         nc.sync.dma_start(out_rows[:, 2:4, HALF:S], y[1][:, 2:4, :])
 
-        yb0 = keep.tile([P, QUARTER * PACK], BF16, name="yb0", tag="wb11", align_bytes=64)
-        yb1 = keep.tile([P, QUARTER * PACK], BF16, name="yb1", tag="scaled3", align_bytes=64)
+        yb0 = keep.tile([P, QUARTER * PACK], BF16, name="yb0", align_bytes=64)
+        yb1 = keep.tile([P, QUARTER * PACK], BF16, name="yb1", tag="scaled_last0", align_bytes=64)
         yb2 = keep.tile([P, QUARTER * PACK], BF16, name="yb2", align_bytes=64)
         y_codes = keep.tile([P, S], U32, name="y_codes", align_bytes=64)
 
@@ -186,14 +204,16 @@ def tile_picked_zfilm_silu_po_kernel(tc, x_words, x_scales, w1, w2, feat, offs, 
         def store_words(a, b):
             nc.sync.dma_start(out_words[:, PACK * a : PACK * b].bitcast(I32), y_codes[:, a:b].bitcast(I32))
 
-        nc.vector.tensor_copy(interleaved(yb0[:]), by_runs(y[0], 0))
+        nc.gpsimd.tensor_scalar(
+            yb0[:].rearrange("p (s t) -> p s t", t=PACK), y[0][:, :, 0:QUARTER].rearrange("p t s -> p s t"), 1.0, 0.0, MULT, ADD
+        )
         nc.vector.tensor_copy(interleaved(yb1[:]), by_runs(y[0], 1))
-        quantise_y(0, yb0)
-        quantise_y(1, yb1)
-        store_words(0, HALF)
         nc.vector.tensor_copy(interleaved(yb2[:]), by_runs(y[1], 0))
-        quantise_y(3, yb3)
+        quantise_y(1, yb1)
+        quantise_y(0, yb0)
+        store_words(0, HALF)
         quantise_y(2, yb2)
+        quantise_y(3, yb3)
         store_words(HALF, S)
         for q in range(4):
             queue = nc.scalar if q % 2 == 0 else nc.sync

@@ -24,6 +24,7 @@ QUARTER = S // 4
 CHUNKS = 4
 PER_COLUMN = 16
 SHARE = 40
+EARLY = 48
 RUN = 2
 
 
@@ -159,8 +160,8 @@ def tile_picked_zfilm_silu_po_kernel(tc, x_words, x_scales, w1, w2, feat, offs, 
         nc.scalar.activation(g_plus_1[:, 0, :], g_banks[1][:, 1, :], COPY, bias=1.0)
         nc.scalar.activation(g_plus_1[:, 1, :], g_banks[2][:, 1, :], COPY, bias=1.0)
         nc.scalar.activation(g_plus_1[:, 2:4, :], g_banks[3][:], COPY, bias=1.0)
-        scaled_slice3 = keep.tile([P, HALF], F32, name="scaled_slice3", tag="wb11", align_bytes=64)
-        nc.gpsimd.tensor_tensor(scaled_slice3[:], g_plus_1[:, 0, :], feat_sb[0, 2][:, 1, :], MULT)
+        scaled[1] = keep.tile([P, 2, HALF], F32, name="scaled1", tag="wb11", align_bytes=64)
+        nc.gpsimd.tensor_tensor(scaled[1][:, 1, :], g_plus_1[:, 0, :], feat_sb[0, 2][:, 1, :], MULT)
         scaled_slice1 = keep.tile([P, HALF], F32, name="scaled_slice1", align_bytes=64)
         nc.gpsimd.tensor_tensor(scaled_slice1[:], g_plus_1[:, 1, :], feat_sb[1, 0][:, 1, :], MULT)
         scaled_last = []
@@ -169,13 +170,9 @@ def tile_picked_zfilm_silu_po_kernel(tc, x_words, x_scales, w1, w2, feat, offs, 
             part = keep.tile([P, 2, QUARTER], F32, name="scaled_last%d" % k, tag="scaled_last%d" % k, align_bytes=64)
             nc.gpsimd.tensor_tensor(part[:], g_plus_1[:, 2:4, cols], feat_sb[1, 2][:, :, cols], MULT)
             scaled_last.append(part)
-        scaled_slice2 = keep.tile([P, HALF], F32, name="scaled_slice2", align_bytes=64)
-        nc.vector.scalar_tensor_tensor(scaled_slice2[:], g_banks[1][:, 0, :], 1.0, feat_sb[0, 2][:, 0, :], ADD, MULT)
+        nc.vector.scalar_tensor_tensor(scaled[1][:, 0, :], g_banks[1][:, 0, :], 1.0, feat_sb[0, 2][:, 0, :], ADD, MULT)
         finish_chunk(0)
-        for e, src in enumerate((scaled_slice2, scaled_slice3)):
-            nc.vector.tensor_tensor(summed[0][:, 2 + e, :], h_banks[1][:, e, :], src[:], ADD)
-        nc.scalar.activation(y[0][:, 2:4, :], summed[0][:, 2:4, :], SILU)
-        nc.sync.dma_start(out_rows[:, 2:4, 0:HALF], y[0][:, 2:4, :])
+        finish_chunk(1)
         scaled_slice0 = keep.tile([P, HALF], F32, name="scaled_slice0", tag="scaled0", align_bytes=64)
         nc.vector.scalar_tensor_tensor(scaled_slice0[:], g_banks[2][:, 0, :], 1.0, feat_sb[1, 0][:, 0, :], ADD, MULT)
         for e, src in ((1, scaled_slice1), (0, scaled_slice0)):
@@ -192,28 +189,25 @@ def tile_picked_zfilm_silu_po_kernel(tc, x_words, x_scales, w1, w2, feat, offs, 
         nc.scalar.activation(interleaved(yb3[:]), by_runs(summed[1], 1), SILU)
         nc.sync.dma_start(out_rows[:, 2:4, HALF:S], y[1][:, 2:4, :])
 
-        yb0 = keep.tile([P, QUARTER * PACK], BF16, name="yb0", align_bytes=64)
-        yb1 = keep.tile([P, QUARTER * PACK], BF16, name="yb1", tag="scaled_last0", align_bytes=64)
+        yb_first = keep.tile([P, HALF * PACK], BF16, name="yb_first", tag="scaled_slice0x", align_bytes=64)
         yb2 = keep.tile([P, QUARTER * PACK], BF16, name="yb2", align_bytes=64)
         y_codes = keep.tile([P, S], U32, name="y_codes", align_bytes=64)
 
-        def quantise_y(quarter, src):
-            cols = slice(quarter * QUARTER, (quarter + 1) * QUARTER)
-            nc.vector.quantize_mx(out=y_codes[:, cols].bitcast(FP8X4), scales=y_scales[:, cols], in_=src[:])
+        def quantise_y(first, last, src):
+            nc.vector.quantize_mx(out=y_codes[:, first:last].bitcast(FP8X4), scales=y_scales[:, first:last], in_=src)
 
         def store_words(a, b):
             nc.sync.dma_start(out_words[:, PACK * a : PACK * b].bitcast(I32), y_codes[:, a:b].bitcast(I32))
 
         nc.gpsimd.tensor_scalar(
-            yb0[:].rearrange("p (s t) -> p s t", t=PACK), y[0][:, :, 0:QUARTER].rearrange("p t s -> p s t"), 1.0, 0.0, MULT, ADD
+            yb_first[:, 0 : PACK * EARLY].rearrange("p (s t) -> p s t", t=PACK), y[0][:, :, 0:EARLY].rearrange("p t s -> p s t"), 1.0, 0.0, MULT, ADD
         )
-        nc.vector.tensor_copy(interleaved(yb1[:]), by_runs(y[0], 1))
+        nc.vector.tensor_copy(interleaved(yb_first[:, PACK * EARLY :]), y[0][:, :, EARLY:].rearrange("p t (a i) -> p a t i", i=RUN))
         nc.vector.tensor_copy(interleaved(yb2[:]), by_runs(y[1], 0))
-        quantise_y(1, yb1)
-        quantise_y(0, yb0)
+        quantise_y(0, HALF, yb_first[:])
         store_words(0, HALF)
-        quantise_y(2, yb2)
-        quantise_y(3, yb3)
+        quantise_y(HALF, HALF + QUARTER, yb2[:])
+        quantise_y(HALF + QUARTER, S, yb3[:])
         store_words(HALF, S)
         for q in range(4):
             queue = nc.scalar if q % 2 == 0 else nc.sync

@@ -54,7 +54,7 @@ def tile_picked_zfilm_silu_po_kernel(tc, x_words, x_scales, w1, w2, feat, offs, 
             w2_raw.append(raw)
         feat_rows = feat.rearrange("(p t) s -> p t s", t=PACK)
         feat_sb = {}
-        for h, first, last in ((0, 0, 2), (0, 2, 4), (1, 0, 2), (1, 2, 4)):
+        for h, first, last in ((0, 0, 2), (0, 2, 3), (0, 3, 4), (1, 0, 4)):
             f = keep.tile([P, last - first, HALF], F32, name="feat%d%d" % (h, first), align_bytes=64)
             nc.sync.dma_start(f[:], feat_rows[:, first:last, h * HALF : (h + 1) * HALF])
             feat_sb[h, first] = f
@@ -158,32 +158,30 @@ def tile_picked_zfilm_silu_po_kernel(tc, x_words, x_scales, w1, w2, feat, offs, 
 
         g_plus_1 = keep.tile([P, 4, HALF], F32, name="g_plus_1", tag="w2_raw1", align_bytes=64)
         nc.scalar.activation(g_plus_1[:, 0, :], g_banks[1][:, 1, :], COPY, bias=1.0)
-        nc.scalar.activation(g_plus_1[:, 1, :], g_banks[2][:, 1, :], COPY, bias=1.0)
+        nc.scalar.activation(g_plus_1[:, 1, 0:QUARTER], g_banks[2][:, 1, 0:QUARTER], COPY, bias=1.0)
         nc.scalar.activation(g_plus_1[:, 2:4, :], g_banks[3][:], COPY, bias=1.0)
         scaled[1] = keep.tile([P, 2, HALF], F32, name="scaled1", tag="wb11", align_bytes=64)
-        nc.gpsimd.tensor_tensor(scaled[1][:, 1, :], g_plus_1[:, 0, :], feat_sb[0, 2][:, 1, :], MULT)
-        scaled_slice1 = keep.tile([P, HALF], F32, name="scaled_slice1", align_bytes=64)
-        nc.gpsimd.tensor_tensor(scaled_slice1[:], g_plus_1[:, 1, :], feat_sb[1, 0][:, 1, :], MULT)
-        scaled_last = []
-        for k in range(2):
-            cols = slice(k * QUARTER, (k + 1) * QUARTER)
-            part = keep.tile([P, 2, QUARTER], F32, name="scaled_last%d" % k, tag="scaled_last%d" % k, align_bytes=64)
-            nc.gpsimd.tensor_tensor(part[:], g_plus_1[:, 2:4, cols], feat_sb[1, 2][:, :, cols], MULT)
-            scaled_last.append(part)
+        nc.gpsimd.tensor_tensor(scaled[1][:, 1, :], g_plus_1[:, 0, :], feat_sb[0, 3][:, 0, :], MULT)
+        first, second = slice(0, QUARTER), slice(QUARTER, HALF)
+        scaled_q2 = keep.tile([P, PACK, QUARTER], F32, name="scaled_q2", align_bytes=64)
+        nc.gpsimd.tensor_tensor(scaled_q2[:, 1:4, :], g_plus_1[:, 1:4, first], feat_sb[1, 0][:, 1:4, first], MULT)
+        scaled_last = keep.tile([P, 2, QUARTER], F32, name="scaled_last", align_bytes=64)
+        nc.gpsimd.tensor_tensor(scaled_last[:], g_plus_1[:, 2:4, second], feat_sb[1, 0][:, 2:4, second], MULT)
         nc.vector.scalar_tensor_tensor(scaled[1][:, 0, :], g_banks[1][:, 0, :], 1.0, feat_sb[0, 2][:, 0, :], ADD, MULT)
         finish_chunk(0)
         finish_chunk(1)
-        scaled_slice0 = keep.tile([P, HALF], F32, name="scaled_slice0", tag="scaled0", align_bytes=64)
-        nc.vector.scalar_tensor_tensor(scaled_slice0[:], g_banks[2][:, 0, :], 1.0, feat_sb[1, 0][:, 0, :], ADD, MULT)
-        for e, src in ((1, scaled_slice1), (0, scaled_slice0)):
-            nc.vector.tensor_tensor(summed[1][:, e, :], h_banks[2][:, e, :], src[:], ADD)
-            nc.scalar.activation(y[1][:, e, :], summed[1][:, e, :], SILU)
+        scaled_q3 = keep.tile([P, 2, QUARTER], F32, name="scaled_q3", tag="scaled0", align_bytes=64)
+        nc.vector.scalar_tensor_tensor(scaled_q2[:, 0, :], g_banks[2][:, 0, first], 1.0, feat_sb[1, 0][:, 0, first], ADD, MULT)
+        nc.vector.scalar_tensor_tensor(scaled_q3[:], g_banks[2][:, :, second], 1.0, feat_sb[1, 0][:, 0:2, second], ADD, MULT)
+        for cols, src in ((first, scaled_q2[:, 0:2, :]), (second, scaled_q3[:])):
+            nc.vector.tensor_tensor(summed[1][:, 0:2, cols], h_banks[2][:, :, cols], src, ADD)
+            nc.scalar.activation(y[1][:, 0:2, cols], summed[1][:, 0:2, cols], SILU)
         nc.sync.dma_start(out_rows[:, 0:2, HALF:S], y[1][:, 0:2, :])
 
         yb3 = keep.tile([P, QUARTER * PACK], BF16, name="yb3", align_bytes=64)
         for k in range(2):
             cols = slice(k * QUARTER, (k + 1) * QUARTER)
-            nc.vector.tensor_tensor(summed[1][:, 2:4, cols], h_banks[3][:, :, cols], scaled_last[k][:], ADD)
+            nc.vector.tensor_tensor(summed[1][:, 2:4, cols], h_banks[3][:, :, cols], (scaled_q2[:, 2:4, :], scaled_last[:])[k], ADD)
         nc.scalar.activation(y[1][:, 2:4, 0:QUARTER], summed[1][:, 2:4, 0:QUARTER], SILU)
         nc.scalar.activation(y[1][:, 2:4, QUARTER:HALF], summed[1][:, 2:4, QUARTER:HALF], SILU)
         nc.scalar.activation(interleaved(yb3[:]), by_runs(summed[1], 1), SILU)

@@ -24,7 +24,7 @@ QUARTER = S // 4
 CHUNKS = 4
 PER_COLUMN = 16
 SHARE = 40
-EARLY = 48
+EARLY = 128
 RUN = 2
 
 
@@ -145,13 +145,6 @@ def tile_picked_zfilm_silu_po_kernel(tc, x_words, x_scales, w1, w2, feat, offs, 
         def by_runs(tile, k):
             return tile[:, :, k * QUARTER : (k + 1) * QUARTER].rearrange("p t (a i) -> p a t i", i=RUN)
 
-        def finish_chunk(c):
-            h, u = divmod(c, 2)
-            rows = slice(2 * u, 2 * u + 2)
-            nc.vector.tensor_tensor(summed[h][:, rows, :], h_banks[c][:], scaled[c][:], ADD)
-            nc.scalar.activation(y[h][:, rows, :], summed[h][:, rows, :], SILU)
-            nc.sync.dma_start(out_rows[:, rows, h * HALF : (h + 1) * HALF], y[h][:, rows, :])
-
         scaled[0] = keep.tile([P, 2, HALF], F32, name="scaled0", tag="scaled0", align_bytes=64)
         nc.vector.scalar_tensor_tensor(scaled[0][:], g_banks[0][:], 1.0, feat_sb[0, 0][:], ADD, MULT)
         h_banks = [product(1, c) for c in range(CHUNKS)]
@@ -168,8 +161,14 @@ def tile_picked_zfilm_silu_po_kernel(tc, x_words, x_scales, w1, w2, feat, offs, 
         scaled_last = keep.tile([P, 2, QUARTER], F32, name="scaled_last", align_bytes=64)
         nc.gpsimd.tensor_tensor(scaled_last[:], g_plus_1[:, 2:4, second], feat_sb[1, 0][:, 2:4, second], MULT)
         nc.vector.scalar_tensor_tensor(scaled[1][:, 0, :], g_banks[1][:, 0, :], 1.0, feat_sb[0, 2][:, 0, :], ADD, MULT)
-        finish_chunk(0)
-        finish_chunk(1)
+        for e in range(2):
+            nc.vector.tensor_tensor(summed[0][:, e, :], h_banks[0][:, e, :], scaled[0][:, e, :], ADD)
+            nc.scalar.activation(y[0][:, e, :], summed[0][:, e, :], SILU)
+        nc.sync.dma_start(out_rows[:, 0:2, 0:HALF], y[0][:, 0:2, :])
+        for cols in (first, second):
+            nc.vector.tensor_tensor(summed[0][:, 2:4, cols], h_banks[1][:, :, cols], scaled[1][:, :, cols], ADD)
+            nc.scalar.activation(y[0][:, 2:4, cols], summed[0][:, 2:4, cols], SILU)
+        nc.sync.dma_start(out_rows[:, 2:4, 0:HALF], y[0][:, 2:4, :])
         scaled_q3 = keep.tile([P, 2, QUARTER], F32, name="scaled_q3", tag="scaled0", align_bytes=64)
         nc.vector.scalar_tensor_tensor(scaled_q2[:, 0, :], g_banks[2][:, 0, first], 1.0, feat_sb[1, 0][:, 0, first], ADD, MULT)
         nc.vector.scalar_tensor_tensor(scaled_q3[:], g_banks[2][:, :, second], 1.0, feat_sb[1, 0][:, 0:2, second], ADD, MULT)

@@ -24,7 +24,7 @@ QUARTER = S // 4
 CHUNKS = 4
 PER_COLUMN = 16
 SHARE = 40
-EARLY = 128
+EARLY = 64
 RUN = 2
 
 
@@ -53,11 +53,10 @@ def tile_picked_zfilm_silu_po_kernel(tc, x_words, x_scales, w1, w2, feat, offs, 
             nc.sync.dma_start(raw[:], w2_rows[:, 2 * pair : 2 * pair + 2, :])
             w2_raw.append(raw)
         feat_rows = feat.rearrange("(p t) s -> p t s", t=PACK)
-        feat_sb = {}
-        for h, first, last in ((0, 0, 2), (0, 2, 3), (0, 3, 4), (1, 0, 4)):
-            f = keep.tile([P, last - first, HALF], F32, name="feat%d%d" % (h, first), align_bytes=64)
-            nc.sync.dma_start(f[:], feat_rows[:, first:last, h * HALF : (h + 1) * HALF])
-            feat_sb[h, first] = f
+        feat_sb = keep.tile([P, PACK, S], F32, name="feat_sb", align_bytes=64)
+        nc.sync.dma_start(feat_sb[:, 0:2, :], feat_rows[:, 0:2, :])
+        for h in range(2):
+            nc.sync.dma_start(feat_sb[:, 2:4, h * HALF : (h + 1) * HALF], feat_rows[:, 2:4, h * HALF : (h + 1) * HALF])
 
         zero = keep.tile([P, 1], F32, name="zero")
         nc.gpsimd.memset(zero[:], 0.0)
@@ -122,7 +121,7 @@ def tile_picked_zfilm_silu_po_kernel(tc, x_words, x_scales, w1, w2, feat, offs, 
                 )
             return bank
 
-        g_banks = {c: product(0, c) for c in range(CHUNKS)}
+        g_banks = {c: product(0, c) for c in (0, 2, 1, 3)}
         round_weight(nc.vector.tensor_copy, 1, w2_raw[0], pairs[0], pairs[0])
         round_weight(nc.scalar.copy, 1, w2_raw[0], pairs[0], pairs[1])
         round_weight(nc.scalar.copy, 1, w2_raw[1], pairs[1], pairs[1], slice(SHARE, P))
@@ -146,21 +145,25 @@ def tile_picked_zfilm_silu_po_kernel(tc, x_words, x_scales, w1, w2, feat, offs, 
             return tile[:, :, k * QUARTER : (k + 1) * QUARTER].rearrange("p t (a i) -> p a t i", i=RUN)
 
         scaled[0] = keep.tile([P, 2, HALF], F32, name="scaled0", tag="scaled0", align_bytes=64)
-        nc.vector.scalar_tensor_tensor(scaled[0][:], g_banks[0][:], 1.0, feat_sb[0, 0][:], ADD, MULT)
+        nc.vector.scalar_tensor_tensor(scaled[0][:], g_banks[0][:], 1.0, feat_sb[:, 0:2, 0:HALF], ADD, MULT)
         h_banks = [product(1, c) for c in range(CHUNKS)]
 
-        g_plus_1 = keep.tile([P, 4, HALF], F32, name="g_plus_1", tag="w2_raw1", align_bytes=64)
-        nc.scalar.activation(g_plus_1[:, 0, :], g_banks[1][:, 1, :], COPY, bias=1.0)
-        nc.scalar.activation(g_plus_1[:, 1, 0:QUARTER], g_banks[2][:, 1, 0:QUARTER], COPY, bias=1.0)
-        nc.scalar.activation(g_plus_1[:, 2:4, :], g_banks[3][:], COPY, bias=1.0)
-        scaled[1] = keep.tile([P, 2, HALF], F32, name="scaled1", tag="wb11", align_bytes=64)
-        nc.gpsimd.tensor_tensor(scaled[1][:, 1, :], g_plus_1[:, 0, :], feat_sb[0, 3][:, 0, :], MULT)
         first, second = slice(0, QUARTER), slice(QUARTER, HALF)
-        scaled_q2 = keep.tile([P, PACK, QUARTER], F32, name="scaled_q2", align_bytes=64)
-        nc.gpsimd.tensor_tensor(scaled_q2[:, 1:4, :], g_plus_1[:, 1:4, first], feat_sb[1, 0][:, 1:4, first], MULT)
-        scaled_last = keep.tile([P, 2, QUARTER], F32, name="scaled_last", align_bytes=64)
-        nc.gpsimd.tensor_tensor(scaled_last[:], g_plus_1[:, 2:4, second], feat_sb[1, 0][:, 2:4, second], MULT)
-        nc.vector.scalar_tensor_tensor(scaled[1][:, 0, :], g_banks[1][:, 0, :], 1.0, feat_sb[0, 2][:, 0, :], ADD, MULT)
+        g_plus_1 = keep.tile([P, 4, HALF], F32, name="g_plus_1", tag="w2_raw1", align_bytes=64)
+        nc.scalar.activation(g_plus_1[:, 0, first], g_banks[2][:, 1, first], COPY, bias=1.0)
+        nc.scalar.activation(g_plus_1[:, 1, :], g_banks[1][:, 1, :], COPY, bias=1.0)
+        nc.scalar.activation(g_plus_1[:, 2:4, :], g_banks[3][:], COPY, bias=1.0)
+        scaled_q2 = keep.tile([P, 2, QUARTER], F32, name="scaled_q2", tag="wb11", align_bytes=64)
+        nc.gpsimd.tensor_tensor(scaled_q2[:, 1, :], g_plus_1[:, 0, first], feat_sb[:, 1, HALF : HALF + QUARTER], MULT)
+        scaled[1] = keep.tile([P, 2, HALF], F32, name="scaled1", align_bytes=64)
+        nc.gpsimd.tensor_tensor(scaled[1][:, 1, :], g_plus_1[:, 1, :], feat_sb[:, 3, 0:HALF], MULT)
+        scaled_last = []
+        for k, cols in enumerate((first, second)):
+            part = keep.tile([P, 2, QUARTER], F32, name="scaled_last%d" % k, align_bytes=64)
+            nc.gpsimd.tensor_tensor(part[:], g_plus_1[:, 2:4, cols], feat_sb[:, 2:4, HALF + cols.start : HALF + cols.stop], MULT)
+            scaled_last.append(part)
+        nc.vector.scalar_tensor_tensor(scaled_q2[:, 0, :], g_banks[2][:, 0, first], 1.0, feat_sb[:, 0, HALF : HALF + QUARTER], ADD, MULT)
+        nc.vector.scalar_tensor_tensor(scaled[1][:, 0, :], g_banks[1][:, 0, :], 1.0, feat_sb[:, 2, 0:HALF], ADD, MULT)
         for e in range(2):
             nc.vector.tensor_tensor(summed[0][:, e, :], h_banks[0][:, e, :], scaled[0][:, e, :], ADD)
             nc.scalar.activation(y[0][:, e, :], summed[0][:, e, :], SILU)
@@ -170,9 +173,8 @@ def tile_picked_zfilm_silu_po_kernel(tc, x_words, x_scales, w1, w2, feat, offs, 
             nc.scalar.activation(y[0][:, 2:4, cols], summed[0][:, 2:4, cols], SILU)
         nc.sync.dma_start(out_rows[:, 2:4, 0:HALF], y[0][:, 2:4, :])
         scaled_q3 = keep.tile([P, 2, QUARTER], F32, name="scaled_q3", tag="scaled0", align_bytes=64)
-        nc.vector.scalar_tensor_tensor(scaled_q2[:, 0, :], g_banks[2][:, 0, first], 1.0, feat_sb[1, 0][:, 0, first], ADD, MULT)
-        nc.vector.scalar_tensor_tensor(scaled_q3[:], g_banks[2][:, :, second], 1.0, feat_sb[1, 0][:, 0:2, second], ADD, MULT)
-        for cols, src in ((first, scaled_q2[:, 0:2, :]), (second, scaled_q3[:])):
+        nc.vector.scalar_tensor_tensor(scaled_q3[:], g_banks[2][:, :, second], 1.0, feat_sb[:, 0:2, HALF + QUARTER : S], ADD, MULT)
+        for cols, src in ((first, scaled_q2[:]), (second, scaled_q3[:])):
             nc.vector.tensor_tensor(summed[1][:, 0:2, cols], h_banks[2][:, :, cols], src, ADD)
             nc.scalar.activation(y[1][:, 0:2, cols], summed[1][:, 0:2, cols], SILU)
         nc.sync.dma_start(out_rows[:, 0:2, HALF:S], y[1][:, 0:2, :])
@@ -180,7 +182,7 @@ def tile_picked_zfilm_silu_po_kernel(tc, x_words, x_scales, w1, w2, feat, offs, 
         yb3 = keep.tile([P, QUARTER * PACK], BF16, name="yb3", align_bytes=64)
         for k in range(2):
             cols = slice(k * QUARTER, (k + 1) * QUARTER)
-            nc.vector.tensor_tensor(summed[1][:, 2:4, cols], h_banks[3][:, :, cols], (scaled_q2[:, 2:4, :], scaled_last[:])[k], ADD)
+            nc.vector.tensor_tensor(summed[1][:, 2:4, cols], h_banks[3][:, :, cols], scaled_last[k][:], ADD)
         nc.scalar.activation(y[1][:, 2:4, 0:QUARTER], summed[1][:, 2:4, 0:QUARTER], SILU)
         nc.scalar.activation(y[1][:, 2:4, QUARTER:HALF], summed[1][:, 2:4, QUARTER:HALF], SILU)
         nc.scalar.activation(interleaved(yb3[:]), by_runs(summed[1], 1), SILU)

@@ -55,8 +55,8 @@ def tile_picked_zfilm_silu_po_kernel(tc, x_words, x_scales, w1, w2, feat, offs, 
         feat_rows = feat.rearrange("(p t) s -> p t s", t=PACK)
         feat_sb = keep.tile([P, PACK, S], F32, name="feat_sb", align_bytes=64)
         nc.sync.dma_start(feat_sb[:, 0:2, :], feat_rows[:, 0:2, :])
-        for h in range(2):
-            nc.sync.dma_start(feat_sb[:, 2:4, h * HALF : (h + 1) * HALF], feat_rows[:, 2:4, h * HALF : (h + 1) * HALF])
+        for rows, cols in ((slice(2, 3), slice(0, S)), (slice(3, 4), slice(0, HALF)), (slice(3, 4), slice(HALF, S))):
+            nc.sync.dma_start(feat_sb[:, rows, cols], feat_rows[:, rows, cols])
 
         zero = keep.tile([P, 1], F32, name="zero")
         nc.gpsimd.memset(zero[:], 0.0)
@@ -163,6 +163,8 @@ def tile_picked_zfilm_silu_po_kernel(tc, x_words, x_scales, w1, w2, feat, offs, 
             nc.gpsimd.tensor_tensor(part[:], g_plus_1[:, 2:4, cols], feat_sb[:, 2:4, HALF + cols.start : HALF + cols.stop], MULT)
             scaled_last.append(part)
         nc.vector.scalar_tensor_tensor(scaled_q2[:, 0, :], g_banks[2][:, 0, first], 1.0, feat_sb[:, 0, HALF : HALF + QUARTER], ADD, MULT)
+        scaled_q3 = keep.tile([P, 2, QUARTER], F32, name="scaled_q3", align_bytes=64)
+        nc.vector.scalar_tensor_tensor(scaled_q3[:], g_banks[2][:, :, second], 1.0, feat_sb[:, 0:2, HALF + QUARTER : S], ADD, MULT)
         nc.vector.scalar_tensor_tensor(scaled[1][:, 0, :], g_banks[1][:, 0, :], 1.0, feat_sb[:, 2, 0:HALF], ADD, MULT)
         for e in range(2):
             nc.vector.tensor_tensor(summed[0][:, e, :], h_banks[0][:, e, :], scaled[0][:, e, :], ADD)
@@ -172,8 +174,6 @@ def tile_picked_zfilm_silu_po_kernel(tc, x_words, x_scales, w1, w2, feat, offs, 
             nc.vector.tensor_tensor(summed[0][:, 2:4, cols], h_banks[1][:, :, cols], scaled[1][:, :, cols], ADD)
             nc.scalar.activation(y[0][:, 2:4, cols], summed[0][:, 2:4, cols], SILU)
         nc.sync.dma_start(out_rows[:, 2:4, 0:HALF], y[0][:, 2:4, :])
-        scaled_q3 = keep.tile([P, 2, QUARTER], F32, name="scaled_q3", tag="scaled0", align_bytes=64)
-        nc.vector.scalar_tensor_tensor(scaled_q3[:], g_banks[2][:, :, second], 1.0, feat_sb[:, 0:2, HALF + QUARTER : S], ADD, MULT)
         for cols, src in ((first, scaled_q2[:]), (second, scaled_q3[:])):
             nc.vector.tensor_tensor(summed[1][:, 0:2, cols], h_banks[2][:, :, cols], src, ADD)
             nc.scalar.activation(y[1][:, 0:2, cols], summed[1][:, 0:2, cols], SILU)

@@ -24,7 +24,6 @@ QUARTER = S // 4
 CHUNKS = 4
 PER_COLUMN = 16
 SHARE = 40
-EARLY = 64
 RUN = 2
 
 
@@ -159,7 +158,7 @@ def tile_picked_zfilm_silu_po_kernel(tc, x_words, x_scales, w1, w2, feat, offs, 
         nc.gpsimd.tensor_tensor(scaled[1][:, 1, :], g_plus_1[:, 1, :], feat_sb[:, 3, 0:HALF], MULT)
         scaled_last = []
         for k, cols in enumerate((first, second)):
-            part = keep.tile([P, 2, QUARTER], F32, name="scaled_last%d" % k, align_bytes=64)
+            part = keep.tile([P, 2, QUARTER], F32, name="scaled_last%d" % k, tag="scaled_last%d" % k, align_bytes=64)
             nc.gpsimd.tensor_tensor(part[:], g_plus_1[:, 2:4, cols], feat_sb[:, 2:4, HALF + cols.start : HALF + cols.stop], MULT)
             scaled_last.append(part)
         nc.vector.scalar_tensor_tensor(scaled_q2[:, 0, :], g_banks[2][:, 0, first], 1.0, feat_sb[:, 0, HALF : HALF + QUARTER], ADD, MULT)
@@ -188,7 +187,7 @@ def tile_picked_zfilm_silu_po_kernel(tc, x_words, x_scales, w1, w2, feat, offs, 
         nc.scalar.activation(interleaved(yb3[:]), by_runs(summed[1], 1), SILU)
         nc.sync.dma_start(out_rows[:, 2:4, HALF:S], y[1][:, 2:4, :])
 
-        yb_first = keep.tile([P, HALF * PACK], BF16, name="yb_first", tag="scaled_slice0x", align_bytes=64)
+        yb_first = keep.tile([P, HALF * PACK], BF16, name="yb_first", tag="scaled_last0", align_bytes=64)
         yb2 = keep.tile([P, QUARTER * PACK], BF16, name="yb2", align_bytes=64)
         y_codes = keep.tile([P, S], U32, name="y_codes", align_bytes=64)
 
@@ -198,10 +197,7 @@ def tile_picked_zfilm_silu_po_kernel(tc, x_words, x_scales, w1, w2, feat, offs, 
         def store_words(a, b):
             nc.sync.dma_start(out_words[:, PACK * a : PACK * b].bitcast(I32), y_codes[:, a:b].bitcast(I32))
 
-        nc.gpsimd.tensor_scalar(
-            yb_first[:, 0 : PACK * EARLY].rearrange("p (s t) -> p s t", t=PACK), y[0][:, :, 0:EARLY].rearrange("p t s -> p s t"), 1.0, 0.0, MULT, ADD
-        )
-        nc.vector.tensor_copy(interleaved(yb_first[:, PACK * EARLY :]), y[0][:, :, EARLY:].rearrange("p t (a i) -> p a t i", i=RUN))
+        nc.vector.tensor_copy(interleaved(yb_first[:]), y[0][:].rearrange("p t (a i) -> p a t i", i=RUN))
         nc.vector.tensor_copy(interleaved(yb2[:]), by_runs(y[1], 0))
         quantise_y(0, HALF, yb_first[:])
         store_words(0, HALF)

from contextlib import ExitStack

import concourse.mybir as mybir

T, S, N, K = 2048, 512, 512, 512
FLOPS = 2 * 2 * K * N * S

F32 = mybir.dt.float32
BF16 = mybir.dt.bfloat16
I32 = mybir.dt.int32
U32 = mybir.dt.uint32
U16 = mybir.dt.uint16
U8 = mybir.dt.uint8
FP8X4 = mybir.dt.float8_e4m3fn_x4
ADD = mybir.AluOpType.add
MULT = mybir.AluOpType.mult
COPY = mybir.ActivationFunctionType.Copy
SILU = mybir.ActivationFunctionType.Silu

P = 128
PACK = 4
HALF = S // 2
QUARTER = S // 4
CHUNKS = 4
PER_COLUMN = 16
SHARE = 40
RUN = 2


def tile_picked_zfilm_silu_po_kernel(tc, x_words, x_scales, w1, w2, feat, offs, out_0, out_1, out_2):
    nc = tc.nc
    with ExitStack() as ctx:
        keep = ctx.enter_context(tc.tile_pool(name="keep", bufs=1))
        psum = ctx.enter_context(tc.psum_pool(name="psum", bufs=1))

        w1_raw = keep.tile([P, PACK, N], F32, name="w1_raw", tag="w1_raw", align_bytes=64)
        w1_rows = w1.rearrange("(p j) c -> p j c", j=PACK)
        nc.sync.dma_start(w1_raw[:, 0:2, :], w1_rows[:, 0:2, :])
        offsets = keep.tile([P, S // PER_COLUMN], U16, name="offsets")
        nc.sync.dma_start(offsets[:], offs)
        table_scales = keep.tile([P, T], U8, name="table_scales", align_bytes=64)
        nc.vector.memset(table_scales[:].bitcast(I32), 0)
        for q in range(4):
            nc.sync.dma_start(table_scales[32 * q : 32 * q + 4, :].bitcast(I32), x_scales[0, 4 * q : 4 * q + 4, :].bitcast(I32))
        nc.sync.dma_start(w1_raw[:, 2:4, :], w1_rows[:, 2:4, :])
        table_words = keep.tile([P, T], U32, name="table_words", align_bytes=64)
        nc.sync.dma_start(table_words[:].bitcast(I32), x_words[0].rearrange("p n t -> p (n t)").bitcast(I32))
        w2_rows = w2.rearrange("(p j) c -> p j c", j=PACK)
        w2_raw = []
        for pair in range(2):
            raw = keep.tile([P, 2, N], F32, name="w2_raw%d" % pair, tag="w2_raw%d" % pair, align_bytes=64)
            nc.sync.dma_start(raw[:], w2_rows[:, 2 * pair : 2 * pair + 2, :])
            w2_raw.append(raw)
        feat_rows = feat.rearrange("(p t) s -> p t s", t=PACK)
        feat_sb = keep.tile([P, PACK, S], F32, name="feat_sb", align_bytes=64)
        nc.sync.dma_start(feat_sb[:, 0:2, :], feat_rows[:, 0:2, :])
        for rows, cols in ((slice(2, 3), slice(0, S)), (slice(3, 4), slice(0, HALF)), (slice(3, 4), slice(HALF, S))):
            nc.sync.dma_start(feat_sb[:, rows, cols], feat_rows[:, rows, cols])

        zero = keep.tile([P, 1], F32, name="zero")
        nc.gpsimd.memset(zero[:], 0.0)
        warm = keep.tile([P, 1], F32, name="warm")
        nc.scalar.activation(warm[:], zero[:], SILU)

        picked_scales = keep.tile([P, S], U8, name="picked_scales", align_bytes=64)
        nc.vector.tensor_copy(picked_scales[:], table_scales[:].indirect(offsets[:]))

        w_codes = {}
        w_scales = {}

        rounded = {
            (i, u): keep.tile([P, 2, P * PACK], BF16, name="wb%d%d" % (i, u), tag="wb%d%d" % (i, u), align_bytes=64)
            for i in range(2)
            for u in range(2)
        }
        for key in rounded:
            w_codes[key] = keep.tile([P, 2, P], U32, name="wc%d%d" % key, align_bytes=64)
            w_scales[key] = keep.tile([P, 2, P], U8, name="ws%d%d" % key, align_bytes=64)

        def round_weight(copy, i, raw, rows, slices, ms=slice(0, P)):
            u, first = divmod(slices.start, 2)
            walk = "p j m t -> p m j t" if rows.stop - rows.start == PACK else "p j m t -> p m t j"
            dst = rounded[i, u][:].rearrange("p t (m j) -> p j m t", j=PACK)[:, rows, ms, first : first + slices.stop - slices.start]
            copy(dst.rearrange(walk), raw[:].rearrange("p j (m t) -> p j m t", t=PACK)[:, :, ms, slices].rearrange(walk))

        def quantise_weight(i, slices):
            u, first = divmod(slices.start, 2)
            part = slice(first, first + slices.stop - slices.start)
            nc.vector.quantize_mx(
                out=w_codes[i, u][:, part, :].rearrange("p e m -> p (e m)").bitcast(FP8X4),
                scales=w_scales[i, u][:, part, :].rearrange("p e m -> p (e m)"),
                in_=rounded[i, u][:, part, :].rearrange("p e c -> p (e c)"),
            )

        pairs = (slice(0, 2), slice(2, 4))
        round_weight(nc.vector.tensor_copy, 0, w1_raw, slice(0, PACK), pairs[0])
        round_weight(nc.scalar.copy, 0, w1_raw, slice(0, PACK), pairs[1])
        for pair in pairs:
            quantise_weight(0, pair)

        picked_words = []
        for h in range(2):
            entries = offsets[:, h * (HALF // PER_COLUMN) : (h + 1) * (HALF // PER_COLUMN)]
            words = keep.tile([P, HALF], U32, name="picked_words%d" % h, align_bytes=64)
            nc.vector.tensor_copy(words[:], table_words[:].indirect(entries))
            picked_words.append(words)

        def product(i, c):
            bank = psum.tile([P, 2, HALF], F32, name="bank%d%d" % (i, c))
            h, u = divmod(c, 2)
            for e in range(2):
                nc.tensor.matmul_mx(
                    out=bank[:, e, :],
                    lhsT=w_codes[i, u][:, e, :].bitcast(FP8X4),
                    lhsT_scale=w_scales[i, u][:, e, :],
                    rhs=picked_words[h][:].bitcast(FP8X4),
                    rhs_scale=picked_scales[:, h * HALF : (h + 1) * HALF],
                    start=True,
                    stop=True,
                )
            return bank

        g_banks = {c: product(0, c) for c in (0, 2, 1, 3)}
        round_weight(nc.vector.tensor_copy, 1, w2_raw[0], pairs[0], pairs[0])
        round_weight(nc.scalar.copy, 1, w2_raw[0], pairs[0], pairs[1])
        round_weight(nc.scalar.copy, 1, w2_raw[1], pairs[1], pairs[1], slice(SHARE, P))
        round_weight(nc.vector.tensor_copy, 1, w2_raw[1], pairs[1], pairs[0])
        round_weight(nc.vector.tensor_copy, 1, w2_raw[1], pairs[1], pairs[1], slice(0, SHARE))
        for pair in pairs:
            quantise_weight(1, pair)

        y_scales = keep.tile([P, S], U8, name="y_scales", align_bytes=64)
        out_rows = out_0.rearrange("(p t) s -> p t s", t=PACK)
        out_words = out_1[0].rearrange("p n t -> p (n t)")

        scaled = {}
        summed = [keep.tile([P, PACK, HALF], F32, name="summed%d" % h, align_bytes=64) for h in range(2)]
        y = [keep.tile([P, PACK, HALF], F32, name="y%d" % h, align_bytes=64) for h in range(2)]

        def interleaved(ap):
            return ap.rearrange("p (a i t) -> p a t i", i=RUN, t=PACK)

        def by_runs(tile, k):
            return tile[:, :, k * QUARTER : (k + 1) * QUARTER].rearrange("p t (a i) -> p a t i", i=RUN)

        scaled[0] = keep.tile([P, 2, HALF], F32, name="scaled0", tag="scaled0", align_bytes=64)
        nc.vector.scalar_tensor_tensor(scaled[0][:], g_banks[0][:], 1.0, feat_sb[:, 0:2, 0:HALF], ADD, MULT)
        h_banks = [product(1, c) for c in range(CHUNKS)]

        first, second = slice(0, QUARTER), slice(QUARTER, HALF)
        g_plus_1 = keep.tile([P, 4, HALF], F32, name="g_plus_1", tag="w2_raw1", align_bytes=64)
        nc.scalar.activation(g_plus_1[:, 0, first], g_banks[2][:, 1, first], COPY, bias=1.0)
        nc.scalar.activation(g_plus_1[:, 1, :], g_banks[1][:, 1, :], COPY, bias=1.0)
        nc.scalar.activation(g_plus_1[:, 2:4, :], g_banks[3][:], COPY, bias=1.0)
        scaled_q2 = keep.tile([P, 2, QUARTER], F32, name="scaled_q2", tag="wb11", align_bytes=64)
        nc.gpsimd.tensor_tensor(scaled_q2[:, 1, :], g_plus_1[:, 0, first], feat_sb[:, 1, HALF : HALF + QUARTER], MULT)
        scaled[1] = keep.tile([P, 2, HALF], F32, name="scaled1", align_bytes=64)
        nc.gpsimd.tensor_tensor(scaled[1][:, 1, :], g_plus_1[:, 1, :], feat_sb[:, 3, 0:HALF], MULT)
        scaled_last = []
        for k, cols in enumerate((first, second)):
            part = keep.tile([P, 2, QUARTER], F32, name="scaled_last%d" % k, tag="scaled_last%d" % k, align_bytes=64)
            nc.gpsimd.tensor_tensor(part[:], g_plus_1[:, 2:4, cols], feat_sb[:, 2:4, HALF + cols.start : HALF + cols.stop], MULT)
            scaled_last.append(part)
        nc.vector.scalar_tensor_tensor(scaled_q2[:, 0, :], g_banks[2][:, 0, first], 1.0, feat_sb[:, 0, HALF : HALF + QUARTER], ADD, MULT)
        scaled_q3 = keep.tile([P, 2, QUARTER], F32, name="scaled_q3", align_bytes=64)
        nc.vector.scalar_tensor_tensor(scaled_q3[:], g_banks[2][:, :, second], 1.0, feat_sb[:, 0:2, HALF + QUARTER : S], ADD, MULT)
        nc.vector.scalar_tensor_tensor(scaled[1][:, 0, :], g_banks[1][:, 0, :], 1.0, feat_sb[:, 2, 0:HALF], ADD, MULT)
        for e in range(2):
            nc.vector.tensor_tensor(summed[0][:, e, :], h_banks[0][:, e, :], scaled[0][:, e, :], ADD)
            nc.scalar.activation(y[0][:, e, :], summed[0][:, e, :], SILU)
        nc.sync.dma_start(out_rows[:, 0:2, 0:HALF], y[0][:, 0:2, :])
        for cols in (first, second):
            nc.vector.tensor_tensor(summed[0][:, 2:4, cols], h_banks[1][:, :, cols], scaled[1][:, :, cols], ADD)
            nc.scalar.activation(y[0][:, 2:4, cols], summed[0][:, 2:4, cols], SILU)
        nc.sync.dma_start(out_rows[:, 2:4, 0:HALF], y[0][:, 2:4, :])
        for cols, src in ((first, scaled_q2[:]), (second, scaled_q3[:])):
            nc.vector.tensor_tensor(summed[1][:, 0:2, cols], h_banks[2][:, :, cols], src, ADD)
            nc.scalar.activation(y[1][:, 0:2, cols], summed[1][:, 0:2, cols], SILU)
        nc.sync.dma_start(out_rows[:, 0:2, HALF:S], y[1][:, 0:2, :])

        yb3 = keep.tile([P, QUARTER * PACK], BF16, name="yb3", align_bytes=64)
        for k in range(2):
            cols = slice(k * QUARTER, (k + 1) * QUARTER)
            nc.vector.tensor_tensor(summed[1][:, 2:4, cols], h_banks[3][:, :, cols], scaled_last[k][:], ADD)
        nc.scalar.activation(y[1][:, 2:4, 0:QUARTER], summed[1][:, 2:4, 0:QUARTER], SILU)
        nc.scalar.activation(y[1][:, 2:4, QUARTER:HALF], summed[1][:, 2:4, QUARTER:HALF], SILU)
        nc.scalar.activation(interleaved(yb3[:]), by_runs(summed[1], 1), SILU)
        nc.sync.dma_start(out_rows[:, 2:4, HALF:S], y[1][:, 2:4, :])

        yb_first = keep.tile([P, HALF * PACK], BF16, name="yb_first", tag="scaled_last0", align_bytes=64)
        yb2 = keep.tile([P, QUARTER * PACK], BF16, name="yb2", align_bytes=64)
        y_codes = keep.tile([P, S], U32, name="y_codes", align_bytes=64)

        def quantise_y(first, last, src):
            nc.vector.quantize_mx(out=y_codes[:, first:last].bitcast(FP8X4), scales=y_scales[:, first:last], in_=src)

        def store_words(a, b):
            nc.sync.dma_start(out_words[:, PACK * a : PACK * b].bitcast(I32), y_codes[:, a:b].bitcast(I32))

        nc.vector.tensor_copy(interleaved(yb_first[:]), y[0][:].rearrange("p t (a i) -> p a t i", i=RUN))
        nc.vector.tensor_copy(interleaved(yb2[:]), by_runs(y[1], 0))
        quantise_y(0, HALF, yb_first[:])
        store_words(0, HALF)
        quantise_y(HALF, HALF + QUARTER, yb2[:])
        quantise_y(HALF + QUARTER, S, yb3[:])
        store_words(HALF, S)
        for q in range(4):
            queue = nc.scalar if q % 2 == 0 else nc.sync
            queue.dma_start(out_2[0, 4 * q : 4 * q + 4, :].bitcast(I32), y_scales[32 * q : 32 * q + 4, :].bitcast(I32))
